import numpy as np
import ml_dtypes


def mxq(x, axis, fmt="e4m3"):
    dtype, down = {"e4m3": (ml_dtypes.float8_e4m3fn, 7), "e5m2": (ml_dtypes.float8_e5m2, 14)}[fmt]
    v = np.moveaxis(np.asarray(x, np.float32).astype(ml_dtypes.bfloat16).astype(np.float64), axis, -1)
    blocks = v.reshape(v.shape[:-1] + (-1, 32))
    amax = np.abs(blocks).max(-1, keepdims=True)
    byte = np.maximum(np.where(amax > 0, np.frexp(amax)[1] - 1 + 127, 0) - down, 1)
    scale = np.exp2(byte - 127.0)
    codes = (blocks / scale).astype(np.float32).astype(dtype).astype(np.float64)
    return np.moveaxis((codes * scale).reshape(v.shape), -1, axis)


WIDE = False


def mx_kscale(k):
    if not WIDE:
        return np.ones(k)
    levels = np.array([10, -10, 5, -5, 0])
    if k % 512:
        return np.exp2(np.random.permutation(np.resize(levels, k // 32))).repeat(32)
    a = np.empty((k // 512, 16))
    for p in range(k // 512):
        a[p, :8] = np.random.permutation(np.resize(levels, 8))
        for g in range(8):
            far = levels[np.abs(levels - a[p, g]) >= 10]
            a[p, g + 8] = far[np.random.randint(len(far))]
    return np.exp2(a.ravel()).repeat(32)


def f64(x):
    return np.asarray(x).astype(np.float64)


E2M1 = np.array([0.0, 0.5, 1.0, 1.5, 2.0, 3.0, 4.0, 6.0, -0.0, -0.5, -1.0, -1.5, -2.0, -3.0, -4.0, -6.0])


def pack_weight(w, fmt):
    k, n = w.shape
    w = f64(np.asarray(w, np.float32).astype(ml_dtypes.bfloat16)).reshape(k // 32, 32, n)
    amax = np.abs(w).max(1)
    if fmt == "e4m3":
        byte = np.frexp(amax)[1] - 1 + 127 - 7
    else:
        mant, ex = np.frexp(amax / 6.0)
        byte = np.where(mant > 0.5, ex, ex - 1) + 127
    byte = np.clip(np.where(amax > 0, byte, 1), 1, 254)
    scaled = (w * np.exp2(127.0 - byte)[:, None, :]).reshape(k, n).astype(np.float32)
    by_word = np.ascontiguousarray(scaled.reshape(k // 512, 128, 4, n).transpose(0, 1, 3, 2))
    if fmt == "e4m3":
        words = by_word.astype(ml_dtypes.float8_e4m3fn).view(np.uint8)
    else:
        c = by_word.astype(ml_dtypes.float4_e2m1fn).view(np.uint8) & 0xF
        words = (c[..., 0::2] | (c[..., 1::2] << 4)).reshape(k // 512, 128, 2 * n)
    return np.ascontiguousarray(words), np.ascontiguousarray(byte.astype(np.uint8).reshape(k // 512, 16, n))


def unpack_weight(words, scales, fmt):
    g, _, n = scales.shape
    words = np.ascontiguousarray(words).reshape(g, 128, n, -1)
    if fmt == "e4m3":
        vals = words.view(ml_dtypes.float8_e4m3fn).astype(np.float64)
    else:
        nib = np.empty((g, 128, n, 4), np.uint8)
        nib[..., 0::2] = words & 0xF
        nib[..., 1::2] = words >> 4
        vals = E2M1[nib]
    vals = vals * np.repeat(np.exp2(scales.astype(np.float64) - 127.0), 8, axis=1)[..., None]
    return vals.transpose(0, 1, 3, 2).reshape(g * 512, n)


def planes(y):
    n, m = y.shape
    v = y.astype(np.float32).astype(ml_dtypes.bfloat16).astype(np.float64).reshape(n // 32, 32, m)
    top = np.abs(v).max(1)
    byte = np.clip(np.where(top > 0, np.frexp(top)[1] - 1 + 127 - 7, 1), 1, 254)
    codes = (v * np.exp2(127.0 - byte)[:, None, :]).reshape(n, m).astype(np.float32).astype(ml_dtypes.float8_e4m3fn).view(np.uint8)
    words = codes.reshape(n // 512, 128, 4, m).transpose(0, 1, 3, 2)
    return np.ascontiguousarray(words), np.ascontiguousarray(byte.astype(np.uint8).reshape(n // 512, 16, m))


O, K, R, M, T = 1024, 2560, 512, 1024, 512


def setup_inputs():
    n = np.random.standard_normal
    s = mx_kscale(K)[:, None]
    u = mx_kscale(R)[:, None]
    x = n((K, T)); x[:O] *= 6.0
    w = n((K, M)) / np.sqrt(K) / s; w[:O] /= 2.0
    p_w8 = pack_weight(w[:O], "e4m3")
    p_w4 = pack_weight(w[O:], "e2m1")
    p_up = pack_weight(n((R, M)) / np.sqrt(R) / u, "e2m1")
    return {
        "x": (x * s).astype(np.float32),
        "w8_words": p_w8[0],
        "w8_scales": p_w8[1],
        "w4_words": p_w4[0],
        "w4_scales": p_w4[1],
        "down": (0.3 * n((K, R)) / np.sqrt(K) / s * u.T).astype(np.float32),
        "up_words": p_up[0],
        "up_scales": p_up[1],
        "b": (0.3 * n(1024)).astype(np.float32),
    }


def reference(x, w8_words, w8_scales, w4_words, w4_scales, down, up_words, up_scales, b):
    x_ = mxq(f64(x), 0, "e4m3")
    w8_ = unpack_weight(w8_words, w8_scales, "e4m3")
    w4_ = unpack_weight(w4_words, w4_scales, "e2m1")
    down_ = mxq(f64(down), 0, "e4m3")
    up_ = unpack_weight(up_words, up_scales, "e2m1")
    h_ = mxq(down_.T @ x_, 0, "e4m3")
    y = x_[:O].T @ w8_ + x_[O:].T @ w4_ + h_.T @ up_
    out_0 = y + f64(b)[None, :]
    return (out_0,) + planes(out_0)

@@ -1,0 +1,263 @@
+from contextlib import ExitStack
+
+import concourse.mybir as mybir
+from concourse.masks import make_identity
+
+O, K, R, M, T = 1024, 2560, 512, 1024, 512
+FLOPS = 2 * T * (K * M + K * R + R * M)
+
+F32 = mybir.dt.float32
+BF16 = mybir.dt.bfloat16
+I32 = mybir.dt.int32
+U32 = mybir.dt.uint32
+U8 = mybir.dt.uint8
+FP8X4 = mybir.dt.float8_e4m3fn_x4
+FP4X4 = mybir.dt.float4_e2m1fn_x4
+
+P = 128
+PACK = 4
+K_PASS = P * PACK
+PASSES = K // K_PASS
+PASSES8 = O // K_PASS
+PASSES4 = PASSES - PASSES8
+HALF = 512
+SCALAR_SHARE = 48
+
+
+def tile_mix_three_tm_pl_bias_kernel(
+    tc, x, w8_words, w8_scales, w4_words, w4_scales, down, up_words, up_scales, b, out_0, out_1, out_2
+):
+    nc = tc.nc
+    with ExitStack() as ctx:
+        keep = ctx.enter_context(tc.tile_pool(name="keep", bufs=1))
+        stage = ctx.enter_context(tc.tile_pool(name="stage", bufs=3))
+        psum = ctx.enter_context(tc.psum_pool(name="psum", bufs=1))
+        ctx.enter_context(tc.manual_schedule())
+
+        def kept(name, shape, dtype):
+            return keep.tile(shape, dtype, name=name, align_bytes=64)
+
+        x_raw = [kept("x_raw%d" % g, [P, PACK, T], F32) for g in range(PASSES)]
+        d_raw = [kept("d_raw%d" % g, [P, PACK, R], F32) for g in range(PASSES)]
+        x_codes = [kept("x_codes%d" % g, [P, T], U32) for g in range(PASSES)]
+        x_plane = [kept("x_plane%d" % g, [P, T], U8) for g in range(PASSES)]
+        d_codes = [kept("d_codes%d" % g, [P, R], U32) for g in range(PASSES)]
+        d_plane = [kept("d_plane%d" % g, [P, R], U8) for g in range(PASSES)]
+        w8_codes = [kept("w8_codes%d" % h, [P, PASSES8, HALF], U32) for h in range(2)]
+        w4_codes = [kept("w4_codes%d" % h, [P, PASSES4, 2 * HALF], U8) for h in range(2)]
+        up_codes = kept("up_codes", [P, 2 * M], U8)
+        w8_plane = kept("w8_plane", [P, PASSES8, M], U8)
+        w4_plane = [kept("w4_plane%d" % h, [P, PASSES4, HALF], U8) for h in range(2)]
+        up_plane = kept("up_plane", [P, 1, M], U8)
+        ident = kept("ident", [P, P], F32)
+        b_cols = kept("b_cols", [P, 2, PACK], F32)
+        bias = kept("bias", [P, M], F32)
+        h_rows = kept("h_rows", [P, PACK, T], BF16)
+        h_grouped = kept("h_grouped", [P, T, PACK], BF16)
+        h_codes = kept("h_codes", [P, T], U32)
+        h_plane = kept("h_plane", [P, T], U8)
+        result = [kept("result%d" % h, [P, PACK, HALF], F32) for h in range(2)]
+        o_grouped = [kept("o_grouped%d" % h, [P, HALF, PACK], BF16) for h in range(2)]
+        o_codes = kept("o_codes", [P, M], U32)
+        o_plane = kept("o_plane", [P, M], U8)
+
+        def cols(n, width):
+            return slice(n * width, (n + 1) * width)
+
+        def load_rows(raw, src, g):
+            nc.sync.dma_start(out=raw[g][:], in_=src[cols(g, K_PASS), :].rearrange("(p j) w -> p j w", j=PACK))
+
+        def load_w8(h):
+            words = w8_words.rearrange("a p n i -> p a (n i)")[:, :, cols(h, PACK * HALF)]
+            nc.sync.dma_start(out=w8_codes[h][:].bitcast(I32), in_=words.bitcast(I32))
+
+        def load_w4(h):
+            words = w4_words.rearrange("a p c -> p a c")[:, :, cols(h, 2 * HALF)]
+            nc.sync.dma_start(out=w4_codes[h][:].bitcast(I32), in_=words.bitcast(I32))
+
+        def load_plane(plane, scales, n_cols):
+            rows = scales.rearrange("a (q r) n -> r q a n", r=4)
+            for r in range(4):
+                nc.sync.dma_start(out=plane[:].bitcast(I32)[r:P:32], in_=rows[r][:, :, n_cols].bitcast(I32))
+
+        def cast_and_deal(raw):
+            grouped = stage.tile([P, PACK, P, PACK], BF16, name="grouped", align_bytes=64)
+            dst = grouped[:].rearrange("p i m j -> p m i j")
+            src = raw[:].rearrange("p j (m i) -> p m i j", i=PACK)
+            nc.scalar.copy(out=dst[:, :SCALAR_SHARE], in_=src[:, :SCALAR_SHARE])
+            nc.vector.tensor_copy(out=dst[:, SCALAR_SHARE:], in_=src[:, SCALAR_SHARE:])
+            return grouped[:].rearrange("p i m j -> p (i m j)")
+
+        def quantize(codes, plane, grouped, first, width):
+            nc.vector.quantize_mx(
+                out=codes[:, first : first + width].bitcast(FP8X4),
+                scales=plane[:, first : first + width],
+                in_=grouped,
+            )
+
+        def interleave(copy, grouped, rows, first, width):
+            copy(
+                out=grouped[:, first : first + width, :].rearrange("p (c u) j -> p c j u", u=4),
+                in_=rows[:, :, first : first + width].rearrange("p j (c u) -> p c j u", u=4),
+            )
+
+        def flat(grouped, first, width):
+            return grouped[:, first : first + width, :].rearrange("p c j -> p (c j)")
+
+        def x_pass(acc, g, i, h):
+            if g < PASSES8:
+                rhs = w8_codes[h][:, g, :].bitcast(FP8X4)
+                rhs_scale = w8_plane[:, g, cols(h, HALF)]
+            else:
+                rhs = w4_codes[h][:, g - PASSES8, :].bitcast(FP4X4)
+                rhs_scale = w4_plane[h][:, g - PASSES8, :]
+            nc.tensor.matmul_mx(
+                out=acc[:],
+                lhsT=x_codes[g][:, cols(i, P)].bitcast(FP8X4),
+                lhsT_scale=x_plane[g][:, cols(i, P)],
+                rhs=rhs,
+                rhs_scale=rhs_scale,
+                start=(g == 0),
+                stop=False,
+            )
+
+        def up_pass(acc, i, h):
+            nc.tensor.matmul_mx(
+                out=acc[:],
+                lhsT=h_codes[:, cols(i, P)].bitcast(FP8X4),
+                lhsT_scale=h_plane[:, cols(i, P)],
+                rhs=up_codes[:, cols(h, 2 * HALF)].bitcast(FP4X4),
+                rhs_scale=up_plane[:, 0, cols(h, HALF)],
+                start=False,
+                stop=True,
+            )
+
+        def add_bias(acc, i, h, first=0, width=HALF):
+            nc.vector.tensor_tensor(
+                out=result[h][:, i, first : first + width],
+                in0=acc[:, first : first + width],
+                in1=bias[:, h * HALF + first : h * HALF + first + width],
+                op=mybir.AluOpType.add,
+            )
+
+        out_rows = out_0.rearrange("(p i) n -> p i n", i=PACK)
+        out_words = out_1[0].rearrange("p n i -> p (n i)").bitcast(I32)
+
+        def store_rows(i, h):
+            nc.sync.dma_start(out=out_rows[:, i, cols(h, HALF)], in_=result[h][:, i, :])
+
+        def store_words(first, width):
+            nc.sync.dma_start(
+                out=out_words[:, first : first + width], in_=o_codes[:, first : first + width].bitcast(I32)
+            )
+
+        nc.scalar.dma_start(out=b_cols[:], in_=b.rearrange("(h p c) -> p h c", h=2, c=PACK))
+        make_identity(nc, ident[:])
+        for plane in (w8_plane, w4_plane[0], w4_plane[1], up_plane):
+            nc.vector.memset(plane[:].bitcast(I32), 0)
+
+        load_rows(x_raw, x, 0)
+        load_rows(d_raw, down, 0)
+        load_w8(0)
+        load_plane(w8_plane, w8_scales, slice(0, M))
+        load_rows(x_raw, x, 1)
+        load_rows(d_raw, down, 1)
+        load_w4(0)
+        load_plane(w4_plane[0], w4_scales, cols(0, HALF))
+        for g in range(2, PASSES):
+            load_rows(x_raw, x, g)
+            load_rows(d_raw, down, g)
+        load_w8(1)
+        load_w4(1)
+        load_plane(w4_plane[1], w4_scales, cols(1, HALF))
+        nc.sync.dma_start(out=up_codes[:].bitcast(I32), in_=up_words[0].bitcast(I32))
+        load_plane(up_plane, up_scales, slice(0, M))
+
+        spread = [psum.tile([P, PACK, P], F32, name="spread%d" % h, tag="bank%d" % (4 + h)) for h in range(2)]
+        for h in range(2):
+            for c in range(PACK):
+                nc.tensor.transpose(spread[h][:, c, :], b_cols[:, h, c : c + 1].to_broadcast([P, P]), ident[:])
+
+        y_low = [psum.tile([P, HALF], F32, name="y_low%d" % i, tag="bank%d" % i) for i in range(PACK)]
+        h_acc = []
+        for g in range(PASSES):
+            grouped = cast_and_deal(x_raw[g])
+            quantize(x_codes[g], x_plane[g], grouped, 0, T)
+            if g == 0:
+                for h, copy in enumerate((nc.scalar.copy, nc.vector.tensor_copy)):
+                    copy(
+                        out=bias[:, cols(h, HALF)].rearrange("t (p c) -> t p c", c=PACK),
+                        in_=spread[h][:].rearrange("t c p -> t p c"),
+                    )
+                h_acc = [psum.tile([P, T], F32, name="h_acc%d" % j, tag="bank%d" % (4 + j)) for j in range(PACK)]
+            for i in range(PACK):
+                x_pass(y_low[i], g, i, 0)
+            grouped = cast_and_deal(d_raw[g])
+            if g < PASSES - 1:
+                quantize(d_codes[g], d_plane[g], grouped, 0, R)
+            else:
+                for j in range(PACK):
+                    quantize(d_codes[g], d_plane[g], grouped[:, cols(j, K_PASS)], j * P, P)
+            for j in range(PACK):
+                nc.tensor.matmul_mx(
+                    out=h_acc[j][:],
+                    lhsT=d_codes[g][:, cols(j, P)].bitcast(FP8X4),
+                    lhsT_scale=d_plane[g][:, cols(j, P)],
+                    rhs=x_codes[g][:].bitcast(FP8X4),
+                    rhs_scale=x_plane[g][:],
+                    start=(g == 0),
+                    stop=(g == PASSES - 1),
+                )
+
+        for j in range(PACK):
+            copy = nc.scalar.copy if j % 2 == 0 else nc.vector.tensor_copy
+            copy(out=h_rows[:, j, :], in_=h_acc[j][:])
+        for i in range(PACK):
+            interleave(nc.vector.tensor_copy if i < 2 else nc.scalar.copy, h_grouped, h_rows, i * P, P)
+        for i in range(PACK):
+            quantize(h_codes, h_plane, flat(h_grouped, i * P, P), i * P, P)
+
+        y_high = [psum.tile([P, HALF], F32, name="y_high%d" % i, tag="bank%d" % (4 + i)) for i in range(PACK)]
+        for g in range(PASSES):
+            x_pass(y_high[0], g, 0, 1)
+        for g in range(2):
+            x_pass(y_high[1], g, 1, 1)
+        for i in range(PACK):
+            up_pass(y_low[i], i, 0)
+        up_pass(y_high[0], 0, 1)
+        for g in range(2, PASSES):
+            x_pass(y_high[1], g, 1, 1)
+        up_pass(y_high[1], 1, 1)
+        for i in (2, 3):
+            for g in range(PASSES):
+                x_pass(y_high[i], g, i, 1)
+            up_pass(y_high[i], i, 1)
+
+        for i in range(PACK):
+            add_bias(y_low[i], i, 0)
+            store_rows(i, 0)
+        interleave(nc.scalar.copy, o_grouped[0], result[0], 0, 256)
+        for i in range(2):
+            add_bias(y_high[i], i, 1)
+            store_rows(i, 1)
+        interleave(nc.vector.tensor_copy, o_grouped[0], result[0], 256, 256)
+        add_bias(y_high[2], 2, 1)
+        store_rows(2, 1)
+        quantize(o_codes, o_plane, flat(o_grouped[0], 0, HALF), 0, HALF)
+        store_words(0, HALF)
+
+        add_bias(y_high[3], 3, 1, 0, 256)
+        add_bias(y_high[3], 3, 1, 256, 256)
+        store_rows(3, 1)
+        interleave(nc.scalar.copy, o_grouped[1], result[1], 0, 128)
+        interleave(nc.vector.tensor_copy, o_grouped[1], result[1], 128, 128)
+        interleave(nc.vector.tensor_copy, o_grouped[1], result[1], 256, 128)
+        interleave(nc.scalar.copy, o_grouped[1], result[1], 384, 128)
+        for first in (0, 256):
+            quantize(o_codes, o_plane, flat(o_grouped[1], first, 256), HALF + first, 256)
+            store_words(HALF + first, 256)
+        for q in range(4):
+            queue = nc.sync if q < 2 else nc.scalar
+            queue.dma_start(
+                out=out_2[0, 4 * q : 4 * q + 4, :].bitcast(I32), in_=o_plane[:].bitcast(I32)[32 * q : 32 * q + 4, :]
+            )

@@ -21,7 +21,11 @@ PASSES = K // K_PASS
 PASSES8 = O // K_PASS
 PASSES4 = PASSES - PASSES8
 HALF = 512
+QUARTER = 256
 SCALAR_SHARE = 48
+PARK_SHARE = 64
+W8_ROW = 4
+PAIR_SHARE = 42
 
 
 def tile_mix_three_tm_pl_bias_kernel(
@@ -38,22 +42,24 @@ def tile_mix_three_tm_pl_bias_kernel(
             return keep.tile(shape, dtype, name=name, align_bytes=64)
 
         x_raw = [kept("x_raw%d" % g, [P, PACK, T], F32) for g in range(PASSES)]
-        d_raw = [kept("d_raw%d" % g, [P, PACK, R], F32) for g in range(PASSES)]
+        d_raw = [kept("d_raw%d" % g, [P, PACK, R], F32) for g in range(PASSES - 1)]
+        d_last = [kept("d_last%d" % e, [P, 2, R], F32) for e in range(2)]
         x_codes = [kept("x_codes%d" % g, [P, T], U32) for g in range(PASSES)]
         x_plane = [kept("x_plane%d" % g, [P, T], U8) for g in range(PASSES)]
         d_codes = [kept("d_codes%d" % g, [P, R], U32) for g in range(PASSES)]
         d_plane = [kept("d_plane%d" % g, [P, R], U8) for g in range(PASSES)]
-        w8_codes = [kept("w8_codes%d" % h, [P, PASSES8, HALF], U32) for h in range(2)]
-        w4_codes = [kept("w4_codes%d" % h, [P, PASSES4, 2 * HALF], U8) for h in range(2)]
+        w8_low = [kept("w8_low%d" % g, [P, HALF], U32) for g in range(PASSES8)]
+        w8_high = kept("w8_high", [P, PASSES8, HALF], U32)
+        w4_codes = kept("w4_codes", [P, PASSES4, 2 * M], U8)
         up_codes = kept("up_codes", [P, 2 * M], U8)
         w8_plane = kept("w8_plane", [P, PASSES8, M], U8)
-        w4_plane = [kept("w4_plane%d" % h, [P, PASSES4, HALF], U8) for h in range(2)]
+        w4_plane = kept("w4_plane", [P, PASSES4, M], U8)
         up_plane = kept("up_plane", [P, 1, M], U8)
         ident = kept("ident", [P, P], F32)
         b_cols = kept("b_cols", [P, 2, PACK], F32)
         bias = kept("bias", [P, M], F32)
-        h_rows = kept("h_rows", [P, PACK, T], BF16)
-        h_grouped = kept("h_grouped", [P, T, PACK], BF16)
+        parked = kept("parked", [P, PACK, HALF], F32)
+        h_grouped = [kept("h_grouped%d" % i, [P, P, PACK], BF16) for i in range(PACK)]
         h_codes = kept("h_codes", [P, T], U32)
         h_plane = kept("h_plane", [P, T], U8)
         result = [kept("result%d" % h, [P, PACK, HALF], F32) for h in range(2)]
@@ -67,25 +73,19 @@ def tile_mix_three_tm_pl_bias_kernel(
         def load_rows(raw, src, g):
             nc.sync.dma_start(out=raw[g][:], in_=src[cols(g, K_PASS), :].rearrange("(p j) w -> p j w", j=PACK))
 
-        def load_w8(h):
-            words = w8_words.rearrange("a p n i -> p a (n i)")[:, :, cols(h, PACK * HALF)]
-            nc.sync.dma_start(out=w8_codes[h][:].bitcast(I32), in_=words.bitcast(I32))
+        w8_view = w8_words.rearrange("a p n i -> p a (n i)")
 
-        def load_w4(h):
-            words = w4_words.rearrange("a p c -> p a c")[:, :, cols(h, 2 * HALF)]
-            nc.sync.dma_start(out=w4_codes[h][:].bitcast(I32), in_=words.bitcast(I32))
-
-        def load_plane(plane, scales, n_cols):
+        def load_plane(plane, scales, first_row):
             rows = scales.rearrange("a (q r) n -> r q a n", r=4)
             for r in range(4):
-                nc.sync.dma_start(out=plane[:].bitcast(I32)[r:P:32], in_=rows[r][:, :, n_cols].bitcast(I32))
+                nc.sync.dma_start(out=plane[:].bitcast(I32)[first_row + r : P : 32], in_=rows[r].bitcast(I32))
 
-        def cast_and_deal(raw):
+        def cast_and_deal(raw, share):
             grouped = stage.tile([P, PACK, P, PACK], BF16, name="grouped", align_bytes=64)
             dst = grouped[:].rearrange("p i m j -> p m i j")
             src = raw[:].rearrange("p j (m i) -> p m i j", i=PACK)
-            nc.scalar.copy(out=dst[:, :SCALAR_SHARE], in_=src[:, :SCALAR_SHARE])
-            nc.vector.tensor_copy(out=dst[:, SCALAR_SHARE:], in_=src[:, SCALAR_SHARE:])
+            nc.scalar.copy(out=dst[:, :share], in_=src[:, :share])
+            nc.vector.tensor_copy(out=dst[:, share:], in_=src[:, share:])
             return grouped[:].rearrange("p i m j -> p (i m j)")
 
         def quantize(codes, plane, grouped, first, width):
@@ -95,56 +95,65 @@ def tile_mix_three_tm_pl_bias_kernel(
                 in_=grouped,
             )
 
-        def interleave(copy, grouped, rows, first, width):
+        def interleave(copy, h, first, width):
             copy(
-                out=grouped[:, first : first + width, :].rearrange("p (c u) j -> p c j u", u=4),
-                in_=rows[:, :, first : first + width].rearrange("p j (c u) -> p c j u", u=4),
+                out=o_grouped[h][:, first : first + width, :].rearrange("p (c u) j -> p c j u", u=4),
+                in_=result[h][:, :, first : first + width].rearrange("p j (c u) -> p c j u", u=4),
             )
 
-        def flat(grouped, first, width):
-            return grouped[:, first : first + width, :].rearrange("p c j -> p (c j)")
+        def quantize_out(h, first, width):
+            grouped = o_grouped[h][:, first : first + width, :].rearrange("p c j -> p (c j)")
+            quantize(o_codes, o_plane, grouped, h * HALF + first, width)
 
-        def x_pass(acc, g, i, h):
-            if g < PASSES8:
-                rhs = w8_codes[h][:, g, :].bitcast(FP8X4)
-                rhs_scale = w8_plane[:, g, cols(h, HALF)]
-            else:
-                rhs = w4_codes[h][:, g - PASSES8, :].bitcast(FP4X4)
-                rhs_scale = w4_plane[h][:, g - PASSES8, :]
+        def w4_pass(acc, g, i, h, start, stop):
             nc.tensor.matmul_mx(
                 out=acc[:],
                 lhsT=x_codes[g][:, cols(i, P)].bitcast(FP8X4),
                 lhsT_scale=x_plane[g][:, cols(i, P)],
-                rhs=rhs,
-                rhs_scale=rhs_scale,
-                start=(g == 0),
+                rhs=w4_codes[:, g - PASSES8, cols(h, 2 * HALF)].bitcast(FP4X4),
+                rhs_scale=w4_plane[:, g - PASSES8, cols(h, HALF)],
+                start=start,
+                stop=stop,
+            )
+
+        def w8_pass(out, g, i, words, first, width, start):
+            nc.tensor.matmul_mx(
+                out=out,
+                lhsT=x_codes[g][:, cols(i, P)].bitcast(FP8X4),
+                lhsT_scale=x_plane[g][:, cols(i, P)],
+                rhs=words.bitcast(FP8X4),
+                rhs_scale=w8_plane[W8_ROW:, g, first : first + width],
+                start=start,
                 stop=False,
             )
 
-        def up_pass(acc, i, h):
+        def up_pass(out, i, first, width, stop):
             nc.tensor.matmul_mx(
-                out=acc[:],
+                out=out,
                 lhsT=h_codes[:, cols(i, P)].bitcast(FP8X4),
                 lhsT_scale=h_plane[:, cols(i, P)],
-                rhs=up_codes[:, cols(h, 2 * HALF)].bitcast(FP4X4),
-                rhs_scale=up_plane[:, 0, cols(h, HALF)],
+                rhs=up_codes[:, 2 * first : 2 * (first + width)].bitcast(FP4X4),
+                rhs_scale=up_plane[:, 0, first : first + width],
                 start=False,
-                stop=True,
+                stop=stop,
             )
 
-        def add_bias(acc, i, h, first=0, width=HALF):
-            nc.vector.tensor_tensor(
-                out=result[h][:, i, first : first + width],
-                in0=acc[:, first : first + width],
-                in1=bias[:, h * HALF + first : h * HALF + first + width],
-                op=mybir.AluOpType.add,
+        def h_pass(g, i, j):
+            nc.tensor.matmul_mx(
+                out=h_acc[i][:, j, :],
+                lhsT=d_codes[g][:, cols(j, P)].bitcast(FP8X4),
+                lhsT_scale=d_plane[g][:, cols(j, P)],
+                rhs=x_codes[g][:, cols(i, P)].bitcast(FP8X4),
+                rhs_scale=x_plane[g][:, cols(i, P)],
+                start=(g == 0 and j == 0),
+                stop=(g == PASSES - 1 and j == PACK - 1),
             )
+
+        def add(out, acc, other):
+            nc.vector.tensor_tensor(out=out, in0=acc, in1=other, op=mybir.AluOpType.add)
 
         out_rows = out_0.rearrange("(p i) n -> p i n", i=PACK)
         out_words = out_1[0].rearrange("p n i -> p (n i)").bitcast(I32)
-
-        def store_rows(i, h):
-            nc.sync.dma_start(out=out_rows[:, i, cols(h, HALF)], in_=result[h][:, i, :])
 
         def store_words(first, width):
             nc.sync.dma_start(
@@ -153,25 +162,27 @@ def tile_mix_three_tm_pl_bias_kernel(
 
         nc.scalar.dma_start(out=b_cols[:], in_=b.rearrange("(h p c) -> p h c", h=2, c=PACK))
         make_identity(nc, ident[:])
-        for plane in (w8_plane, w4_plane[0], w4_plane[1], up_plane):
+        for plane in (w4_plane, w8_plane, up_plane):
             nc.vector.memset(plane[:].bitcast(I32), 0)
 
+        load_rows(x_raw, x, 2)
+        nc.sync.dma_start(out=w4_codes[:].bitcast(I32), in_=w4_words.rearrange("a p c -> p a c").bitcast(I32))
+        load_plane(w4_plane, w4_scales, 0)
+        load_rows(x_raw, x, 3)
+        load_rows(x_raw, x, 4)
+        load_plane(w8_plane, w8_scales, W8_ROW)
         load_rows(x_raw, x, 0)
-        load_rows(d_raw, down, 0)
-        load_w8(0)
-        load_plane(w8_plane, w8_scales, slice(0, M))
         load_rows(x_raw, x, 1)
-        load_rows(d_raw, down, 1)
-        load_w4(0)
-        load_plane(w4_plane[0], w4_scales, cols(0, HALF))
-        for g in range(2, PASSES):
-            load_rows(x_raw, x, g)
+        for g in range(PASSES - 1):
             load_rows(d_raw, down, g)
-        load_w8(1)
-        load_w4(1)
-        load_plane(w4_plane[1], w4_scales, cols(1, HALF))
+        last_rows = down[cols(PASSES - 1, K_PASS), :].rearrange("(p j) w -> p j w", j=PACK)
+        for e in range(2):
+            nc.sync.dma_start(out=d_last[e][:], in_=last_rows[:, cols(e, 2), :])
+        for g in range(PASSES8):
+            nc.sync.dma_start(out=w8_low[g][:].bitcast(I32), in_=w8_view[:, g, cols(0, PACK * HALF)].bitcast(I32))
         nc.sync.dma_start(out=up_codes[:].bitcast(I32), in_=up_words[0].bitcast(I32))
-        load_plane(up_plane, up_scales, slice(0, M))
+        load_plane(up_plane, up_scales, 0)
+        nc.sync.dma_start(out=w8_high[:].bitcast(I32), in_=w8_view[:, :, cols(1, PACK * HALF)].bitcast(I32))
 
         spread = [psum.tile([P, PACK, P], F32, name="spread%d" % h, tag="bank%d" % (4 + h)) for h in range(2)]
         for h in range(2):
@@ -179,83 +190,133 @@ def tile_mix_three_tm_pl_bias_kernel(
                 nc.tensor.transpose(spread[h][:, c, :], b_cols[:, h, c : c + 1].to_broadcast([P, P]), ident[:])
 
         y_low = [psum.tile([P, HALF], F32, name="y_low%d" % i, tag="bank%d" % i) for i in range(PACK)]
-        h_acc = []
-        for g in range(PASSES):
-            grouped = cast_and_deal(x_raw[g])
+        y_early = []
+        for g in range(PASSES8, PASSES):
+            grouped = cast_and_deal(x_raw[g], SCALAR_SHARE)
             quantize(x_codes[g], x_plane[g], grouped, 0, T)
-            if g == 0:
+            if g == PASSES8:
                 for h, copy in enumerate((nc.scalar.copy, nc.vector.tensor_copy)):
                     copy(
                         out=bias[:, cols(h, HALF)].rearrange("t (p c) -> t p c", c=PACK),
                         in_=spread[h][:].rearrange("t c p -> t p c"),
                     )
-                h_acc = [psum.tile([P, T], F32, name="h_acc%d" % j, tag="bank%d" % (4 + j)) for j in range(PACK)]
+                y_early = [psum.tile([P, HALF], F32, name="y_early%d" % i, tag="bank%d" % (4 + i)) for i in range(PACK)]
             for i in range(PACK):
-                x_pass(y_low[i], g, i, 0)
-            grouped = cast_and_deal(d_raw[g])
-            if g < PASSES - 1:
-                quantize(d_codes[g], d_plane[g], grouped, 0, R)
-            else:
+                w4_pass(y_early[i], g, i, 1, g == PASSES8, g == PASSES - 1)
+            for i in range(PACK):
+                w4_pass(y_low[i], g, i, 0, g == PASSES8, False)
+
+        for g in range(PASSES8):
+            grouped = cast_and_deal(x_raw[g], PARK_SHARE)
+            for i in (2 * g, 2 * g + 1):
+                add(parked[:, i, :], y_early[i][:], bias[:, cols(1, HALF)])
+            quantize(x_codes[g], x_plane[g], grouped, 0, T)
+
+        h_acc = [psum.tile([P, PACK, P], F32, name="h_acc%d" % i, tag="bank%d" % (4 + i)) for i in range(PACK)]
+        for g in range(PASSES - 1):
+            grouped = cast_and_deal(d_raw[g], SCALAR_SHARE)
+            quantize(d_codes[g], d_plane[g], grouped, 0, R)
+            for i in range(PACK):
                 for j in range(PACK):
-                    quantize(d_codes[g], d_plane[g], grouped[:, cols(j, K_PASS)], j * P, P)
-            for j in range(PACK):
-                nc.tensor.matmul_mx(
-                    out=h_acc[j][:],
-                    lhsT=d_codes[g][:, cols(j, P)].bitcast(FP8X4),
-                    lhsT_scale=d_plane[g][:, cols(j, P)],
-                    rhs=x_codes[g][:].bitcast(FP8X4),
-                    rhs_scale=x_plane[g][:],
-                    start=(g == 0),
-                    stop=(g == PASSES - 1),
-                )
-
-        for j in range(PACK):
-            copy = nc.scalar.copy if j % 2 == 0 else nc.vector.tensor_copy
-            copy(out=h_rows[:, j, :], in_=h_acc[j][:])
-        for i in range(PACK):
-            interleave(nc.vector.tensor_copy if i < 2 else nc.scalar.copy, h_grouped, h_rows, i * P, P)
-        for i in range(PACK):
-            quantize(h_codes, h_plane, flat(h_grouped, i * P, P), i * P, P)
-
-        y_high = [psum.tile([P, HALF], F32, name="y_high%d" % i, tag="bank%d" % (4 + i)) for i in range(PACK)]
-        for g in range(PASSES):
-            x_pass(y_high[0], g, 0, 1)
-        for g in range(2):
-            x_pass(y_high[1], g, 1, 1)
-        for i in range(PACK):
-            up_pass(y_low[i], i, 0)
-        up_pass(y_high[0], 0, 1)
-        for g in range(2, PASSES):
-            x_pass(y_high[1], g, 1, 1)
-        up_pass(y_high[1], 1, 1)
-        for i in (2, 3):
-            for g in range(PASSES):
-                x_pass(y_high[i], g, i, 1)
-            up_pass(y_high[i], i, 1)
-
-        for i in range(PACK):
-            add_bias(y_low[i], i, 0)
-            store_rows(i, 0)
-        interleave(nc.scalar.copy, o_grouped[0], result[0], 0, 256)
+                    h_pass(g, i, j)
+        g = PASSES - 1
+        last = stage.tile([P, PACK, P, PACK], BF16, name="grouped", align_bytes=64)
+        for e in range(2):
+            dst = last[:].rearrange("p i m j -> p m i j")[:, :, :, cols(e, 2)]
+            src = d_last[e][:].rearrange("p j (m i) -> p m i j", i=PACK)
+            nc.scalar.copy(out=dst[:, :PAIR_SHARE], in_=src[:, :PAIR_SHARE])
+            nc.vector.tensor_copy(out=dst[:, PAIR_SHARE:], in_=src[:, PAIR_SHARE:])
+        grouped = last[:].rearrange("p i m j -> p (i m j)")
+        for half in range(2):
+            quantize(d_codes[g], d_plane[g], grouped[:, cols(half, 2 * K_PASS)], half * 2 * P, 2 * P)
         for i in range(2):
-            add_bias(y_high[i], i, 1)
-            store_rows(i, 1)
-        interleave(nc.vector.tensor_copy, o_grouped[0], result[0], 256, 256)
-        add_bias(y_high[2], 2, 1)
-        store_rows(2, 1)
-        quantize(o_codes, o_plane, flat(o_grouped[0], 0, HALF), 0, HALF)
-        store_words(0, HALF)
+            w8_pass(y_low[i][:], 0, i, w8_low[0][:], 0, HALF, False)
+        for i, j in ((0, 0), (0, 1), (1, 0), (1, 1), (0, 2), (0, 3), (1, 2), (1, 3)):
+            h_pass(g, i, j)
+        for i in (2, 3):
+            for j in range(PACK):
+                h_pass(g, i, j)
 
-        add_bias(y_high[3], 3, 1, 0, 256)
-        add_bias(y_high[3], 3, 1, 256, 256)
-        store_rows(3, 1)
-        interleave(nc.scalar.copy, o_grouped[1], result[1], 0, 128)
-        interleave(nc.vector.tensor_copy, o_grouped[1], result[1], 128, 128)
-        interleave(nc.vector.tensor_copy, o_grouped[1], result[1], 256, 128)
-        interleave(nc.scalar.copy, o_grouped[1], result[1], 384, 128)
-        for first in (0, 256):
-            quantize(o_codes, o_plane, flat(o_grouped[1], first, 256), HALF + first, 256)
-            store_words(HALF + first, 256)
+        def h_out(copy, i):
+            copy(out=h_grouped[i][:], in_=h_acc[i][:].rearrange("p j t -> p t j"))
+
+        def h_quantize(i):
+            quantize(h_codes, h_plane, h_grouped[i][:].rearrange("p t j -> p (t j)"), i * P, P)
+
+        def add_low(i, first, width):
+            c = slice(first, first + width)
+            add(result[0][:, i, c], y_low[i][:, c], bias[:, c])
+            if first + width == HALF:
+                nc.sync.dma_start(out=out_rows[:, i, cols(0, HALF)], in_=result[0][:, i, :])
+
+        h_out(nc.scalar.copy, 0)
+        h_out(nc.vector.tensor_copy, 1)
+        h_out(nc.scalar.copy, 2)
+        h_out(nc.scalar.copy, 3)
+        for i in range(3):
+            h_quantize(i)
+
+        def low_w8(i, g):
+            w8_pass(y_low[i][:], g, i, w8_low[g][:], 0, HALF, False)
+
+        def low_up(i):
+            up_pass(y_low[i][:], i, 0, HALF, True)
+
+        low_w8(0, 1)
+        low_w8(1, 1)
+        low_up(0)
+        low_up(1)
+        add_low(0, 0, HALF)
+        h_quantize(3)
+        for i in (2, 3):
+            low_w8(i, 0)
+            low_w8(i, 1)
+            low_up(i)
+        add_low(1, 0, HALF)
+        add_low(2, 0, HALF)
+        add_low(3, 0, QUARTER)
+        interleave(nc.scalar.copy, 0, 0, QUARTER)
+        add_low(3, QUARTER, QUARTER)
+        interleave(nc.scalar.copy, 0, QUARTER, QUARTER)
+
+        def high_bank(bank, slots, first, width):
+            n = len(slots)
+            acc = psum.tile([P, n, width], F32, name="y_high", tag="bank%d" % bank)
+            c = slice(first, first + width)
+            rows = slice(slots[0], slots[0] + n)
+            for g in range(PASSES8):
+                for e, i in enumerate(slots):
+                    w8_pass(acc[:, e, :], g, i, w8_high[:, g, c], HALF + first, width, g == 0 and e == 0)
+            step = HALF if width == HALF else P
+            for e, i in enumerate(slots):
+                for u in range(0, width, step):
+                    up_pass(acc[:, e, u : u + step], i, HALF + first + u, step, e == n - 1 and u + step == width)
+            add(result[1][:, rows, c], acc[:], parked[:, rows, c])
+
+        def store_high(rows, first, width):
+            nc.sync.dma_start(
+                out=out_rows[:, rows, HALF + first : HALF + first + width], in_=result[1][:, rows, first : first + width]
+            )
+
+        for i in range(2):
+            high_bank(4 + i, (i,), 0, HALF)
+            store_high(slice(i, i + 1), 0, HALF)
+        quantize_out(0, 0, QUARTER)
+        high_bank(6, (2, 3), 0, QUARTER)
+        store_high(slice(2, 4), 0, QUARTER)
+        interleave(nc.scalar.copy, 1, 0, P)
+        high_bank(7, (2, 3), QUARTER, P)
+        interleave(nc.scalar.copy, 1, QUARTER, P)
+        interleave(nc.vector.tensor_copy, 1, P, P)
+        high_bank(0, (2, 3), QUARTER + P, P)
+        store_high(slice(2, 4), QUARTER, QUARTER)
+        quantize_out(0, QUARTER, QUARTER)
+        store_words(0, HALF)
+        interleave(nc.vector.tensor_copy, 1, QUARTER + P, P)
+        quantize_out(1, 0, QUARTER)
+        store_words(HALF, QUARTER)
+        quantize_out(1, QUARTER, QUARTER)
+        store_words(HALF + QUARTER, QUARTER)
         for q in range(4):
             queue = nc.sync if q < 2 else nc.scalar
             queue.dma_start(

@@ -24,7 +24,6 @@ HALF = 512
 QUARTER = 256
 SCALAR_SHARE = 48
 PARK_SHARE = 64
-W8_ROW = 4
 PAIR_SHARE = 42
 
 
@@ -75,10 +74,10 @@ def tile_mix_three_tm_pl_bias_kernel(
 
         w8_view = w8_words.rearrange("a p n i -> p a (n i)")
 
-        def load_plane(plane, scales, first_row):
+        def load_plane(plane, scales):
             rows = scales.rearrange("a (q r) n -> r q a n", r=4)
             for r in range(4):
-                nc.sync.dma_start(out=plane[:].bitcast(I32)[first_row + r : P : 32], in_=rows[r].bitcast(I32))
+                nc.sync.dma_start(out=plane[:].bitcast(I32)[r:P:32], in_=rows[r].bitcast(I32))
 
         def cast_and_deal(raw, share):
             grouped = stage.tile([P, PACK, P, PACK], BF16, name="grouped", align_bytes=64)
@@ -122,7 +121,7 @@ def tile_mix_three_tm_pl_bias_kernel(
                 lhsT=x_codes[g][:, cols(i, P)].bitcast(FP8X4),
                 lhsT_scale=x_plane[g][:, cols(i, P)],
                 rhs=words.bitcast(FP8X4),
-                rhs_scale=w8_plane[W8_ROW:, g, first : first + width],
+                rhs_scale=w8_plane[:, g, first : first + width],
                 start=start,
                 stop=False,
             )
@@ -167,10 +166,10 @@ def tile_mix_three_tm_pl_bias_kernel(
 
         load_rows(x_raw, x, 2)
         nc.sync.dma_start(out=w4_codes[:].bitcast(I32), in_=w4_words.rearrange("a p c -> p a c").bitcast(I32))
-        load_plane(w4_plane, w4_scales, 0)
+        load_plane(w4_plane, w4_scales)
         load_rows(x_raw, x, 3)
         load_rows(x_raw, x, 4)
-        load_plane(w8_plane, w8_scales, W8_ROW)
+        load_plane(w8_plane, w8_scales)
         load_rows(x_raw, x, 0)
         load_rows(x_raw, x, 1)
         for g in range(PASSES - 1):
@@ -181,7 +180,7 @@ def tile_mix_three_tm_pl_bias_kernel(
         for g in range(PASSES8):
             nc.sync.dma_start(out=w8_low[g][:].bitcast(I32), in_=w8_view[:, g, cols(0, PACK * HALF)].bitcast(I32))
         nc.sync.dma_start(out=up_codes[:].bitcast(I32), in_=up_words[0].bitcast(I32))
-        load_plane(up_plane, up_scales, 0)
+        load_plane(up_plane, up_scales)
         nc.sync.dma_start(out=w8_high[:].bitcast(I32), in_=w8_view[:, :, cols(1, PACK * HALF)].bitcast(I32))
 
         spread = [psum.tile([P, PACK, P], F32, name="spread%d" % h, tag="bank%d" % (4 + h)) for h in range(2)]

@@ -24,7 +24,7 @@ HALF = 512
 QUARTER = 256
 SCALAR_SHARE = 48
 PARK_SHARE = 64
-PAIR_SHARE = 42
+LAST_SHARE = 42
 
 
 def tile_mix_three_tm_pl_bias_kernel(
@@ -41,8 +41,7 @@ def tile_mix_three_tm_pl_bias_kernel(
             return keep.tile(shape, dtype, name=name, align_bytes=64)
 
         x_raw = [kept("x_raw%d" % g, [P, PACK, T], F32) for g in range(PASSES)]
-        d_raw = [kept("d_raw%d" % g, [P, PACK, R], F32) for g in range(PASSES - 1)]
-        d_last = [kept("d_last%d" % e, [P, 2, R], F32) for e in range(2)]
+        d_raw = [kept("d_raw%d" % g, [P, PACK, R], F32) for g in range(PASSES)]
         x_codes = [kept("x_codes%d" % g, [P, T], U32) for g in range(PASSES)]
         x_plane = [kept("x_plane%d" % g, [P, T], U8) for g in range(PASSES)]
         d_codes = [kept("d_codes%d" % g, [P, R], U32) for g in range(PASSES)]
@@ -51,11 +50,11 @@ def tile_mix_three_tm_pl_bias_kernel(
         w8_high = kept("w8_high", [P, PASSES8, HALF], U32)
         w4_codes = kept("w4_codes", [P, PASSES4, 2 * M], U8)
         up_codes = kept("up_codes", [P, 2 * M], U8)
-        w8_plane = kept("w8_plane", [P, PASSES8, M], U8)
+        w8_plane = [kept("w8_plane%d" % h, [P, PASSES8, HALF], U8) for h in range(2)]
         w4_plane = kept("w4_plane", [P, PASSES4, M], U8)
         up_plane = kept("up_plane", [P, 1, M], U8)
         ident = kept("ident", [P, P], F32)
-        b_cols = kept("b_cols", [P, 2, PACK], F32)
+        b_cols = kept("b_cols", [P, 2 * PACK], F32)
         bias = kept("bias", [P, M], F32)
         parked = kept("parked", [P, PACK, HALF], F32)
         h_grouped = [kept("h_grouped%d" % i, [P, P, PACK], BF16) for i in range(PACK)]
@@ -74,10 +73,10 @@ def tile_mix_three_tm_pl_bias_kernel(
 
         w8_view = w8_words.rearrange("a p n i -> p a (n i)")
 
-        def load_plane(plane, scales):
+        def load_plane(plane, scales, n_cols=slice(0, M)):
             rows = scales.rearrange("a (q r) n -> r q a n", r=4)
             for r in range(4):
-                nc.sync.dma_start(out=plane[:].bitcast(I32)[r:P:32], in_=rows[r].bitcast(I32))
+                nc.sync.dma_start(out=plane[:].bitcast(I32)[r:P:32], in_=rows[r][:, :, n_cols].bitcast(I32))
 
         def cast_and_deal(raw, share):
             grouped = stage.tile([P, PACK, P, PACK], BF16, name="grouped", align_bytes=64)
@@ -121,7 +120,7 @@ def tile_mix_three_tm_pl_bias_kernel(
                 lhsT=x_codes[g][:, cols(i, P)].bitcast(FP8X4),
                 lhsT_scale=x_plane[g][:, cols(i, P)],
                 rhs=words.bitcast(FP8X4),
-                rhs_scale=w8_plane[:, g, first : first + width],
+                rhs_scale=w8_plane[first // HALF][:, g, first % HALF : first % HALF + width],
                 start=start,
                 stop=False,
             )
@@ -159,9 +158,9 @@ def tile_mix_three_tm_pl_bias_kernel(
                 out=out_words[:, first : first + width], in_=o_codes[:, first : first + width].bitcast(I32)
             )
 
-        nc.scalar.dma_start(out=b_cols[:], in_=b.rearrange("(h p c) -> p h c", h=2, c=PACK))
+        nc.scalar.dma_start(out=b_cols[:], in_=b.rearrange("(p c) -> p c", p=P))
         make_identity(nc, ident[:])
-        for plane in (w4_plane, w8_plane, up_plane):
+        for plane in (w4_plane, w8_plane[0], up_plane, w8_plane[1]):
             nc.vector.memset(plane[:].bitcast(I32), 0)
 
         load_rows(x_raw, x, 2)
@@ -169,24 +168,22 @@ def tile_mix_three_tm_pl_bias_kernel(
         load_plane(w4_plane, w4_scales)
         load_rows(x_raw, x, 3)
         load_rows(x_raw, x, 4)
-        load_plane(w8_plane, w8_scales)
+        load_plane(w8_plane[0], w8_scales, cols(0, HALF))
         load_rows(x_raw, x, 0)
         load_rows(x_raw, x, 1)
-        for g in range(PASSES - 1):
+        for g in range(PASSES):
             load_rows(d_raw, down, g)
-        last_rows = down[cols(PASSES - 1, K_PASS), :].rearrange("(p j) w -> p j w", j=PACK)
-        for e in range(2):
-            nc.sync.dma_start(out=d_last[e][:], in_=last_rows[:, cols(e, 2), :])
-        for g in range(PASSES8):
-            nc.sync.dma_start(out=w8_low[g][:].bitcast(I32), in_=w8_view[:, g, cols(0, PACK * HALF)].bitcast(I32))
-        nc.sync.dma_start(out=up_codes[:].bitcast(I32), in_=up_words[0].bitcast(I32))
+        nc.sync.dma_start(out=w8_low[0][:].bitcast(I32), in_=w8_view[:, 0, cols(0, PACK * HALF)].bitcast(I32))
         load_plane(up_plane, up_scales)
+        nc.sync.dma_start(out=w8_low[1][:].bitcast(I32), in_=w8_view[:, 1, cols(0, PACK * HALF)].bitcast(I32))
+        nc.sync.dma_start(out=up_codes[:].bitcast(I32), in_=up_words[0].bitcast(I32))
         nc.sync.dma_start(out=w8_high[:].bitcast(I32), in_=w8_view[:, :, cols(1, PACK * HALF)].bitcast(I32))
+        load_plane(w8_plane[1], w8_scales, cols(1, HALF))
 
         spread = [psum.tile([P, PACK, P], F32, name="spread%d" % h, tag="bank%d" % (4 + h)) for h in range(2)]
         for h in range(2):
             for c in range(PACK):
-                nc.tensor.transpose(spread[h][:, c, :], b_cols[:, h, c : c + 1].to_broadcast([P, P]), ident[:])
+                nc.tensor.transpose(spread[h][:, c, :], b_cols[:, PACK * h + c : PACK * h + c + 1].to_broadcast([P, P]), ident[:])
 
         y_low = [psum.tile([P, HALF], F32, name="y_low%d" % i, tag="bank%d" % i) for i in range(PACK)]
         y_early = []
@@ -196,7 +193,7 @@ def tile_mix_three_tm_pl_bias_kernel(
             if g == PASSES8:
                 for h, copy in enumerate((nc.scalar.copy, nc.vector.tensor_copy)):
                     copy(
-                        out=bias[:, cols(h, HALF)].rearrange("t (p c) -> t p c", c=PACK),
+                        out=bias[:].rearrange("t (p h c) -> t h p c", h=2, c=PACK)[:, h],
                         in_=spread[h][:].rearrange("t c p -> t p c"),
                     )
                 y_early = [psum.tile([P, HALF], F32, name="y_early%d" % i, tag="bank%d" % (4 + i)) for i in range(PACK)]
@@ -219,16 +216,10 @@ def tile_mix_three_tm_pl_bias_kernel(
                 for j in range(PACK):
                     h_pass(g, i, j)
         g = PASSES - 1
-        last = stage.tile([P, PACK, P, PACK], BF16, name="grouped", align_bytes=64)
-        for e in range(2):
-            dst = last[:].rearrange("p i m j -> p m i j")[:, :, :, cols(e, 2)]
-            src = d_last[e][:].rearrange("p j (m i) -> p m i j", i=PACK)
-            nc.scalar.copy(out=dst[:, :PAIR_SHARE], in_=src[:, :PAIR_SHARE])
-            nc.vector.tensor_copy(out=dst[:, PAIR_SHARE:], in_=src[:, PAIR_SHARE:])
-        grouped = last[:].rearrange("p i m j -> p (i m j)")
+        grouped = cast_and_deal(d_raw[g], LAST_SHARE)
         for half in range(2):
             quantize(d_codes[g], d_plane[g], grouped[:, cols(half, 2 * K_PASS)], half * 2 * P, 2 * P)
-        for i in range(2):
+        for i in range(PACK):
             w8_pass(y_low[i][:], 0, i, w8_low[0][:], 0, HALF, False)
         for i, j in ((0, 0), (0, 1), (1, 0), (1, 1), (0, 2), (0, 3), (1, 2), (1, 3)):
             h_pass(g, i, j)
@@ -268,7 +259,6 @@ def tile_mix_three_tm_pl_bias_kernel(
         add_low(0, 0, HALF)
         h_quantize(3)
         for i in (2, 3):
-            low_w8(i, 0)
             low_w8(i, 1)
             low_up(i)
         add_low(1, 0, HALF)
@@ -306,11 +296,11 @@ def tile_mix_three_tm_pl_bias_kernel(
         interleave(nc.scalar.copy, 1, 0, P)
         high_bank(7, (2, 3), QUARTER, P)
         interleave(nc.scalar.copy, 1, QUARTER, P)
-        interleave(nc.vector.tensor_copy, 1, P, P)
-        high_bank(0, (2, 3), QUARTER + P, P)
-        store_high(slice(2, 4), QUARTER, QUARTER)
         quantize_out(0, QUARTER, QUARTER)
         store_words(0, HALF)
+        high_bank(0, (2, 3), QUARTER + P, P)
+        store_high(slice(2, 4), QUARTER, QUARTER)
+        interleave(nc.vector.tensor_copy, 1, P, P)
         interleave(nc.vector.tensor_copy, 1, QUARTER + P, P)
         quantize_out(1, 0, QUARTER)
         store_words(HALF, QUARTER)

@@ -80,8 +80,8 @@ def tile_mix_three_tm_pl_bias_kernel(
 
         def cast_and_deal(raw, share):
             grouped = stage.tile([P, PACK, P, PACK], BF16, name="grouped", align_bytes=64)
-            dst = grouped[:].rearrange("p i m j -> p m i j")
-            src = raw[:].rearrange("p j (m i) -> p m i j", i=PACK)
+            dst = grouped[:].rearrange("p i m j -> p m j i")
+            src = raw[:].rearrange("p j (m i) -> p m j i", i=PACK)
             nc.scalar.copy(out=dst[:, :share], in_=src[:, :share])
             nc.vector.tensor_copy(out=dst[:, share:], in_=src[:, share:])
             return grouped[:].rearrange("p i m j -> p (i m j)")
@@ -209,12 +209,18 @@ def tile_mix_three_tm_pl_bias_kernel(
             quantize(x_codes[g], x_plane[g], grouped, 0, T)
 
         h_acc = [psum.tile([P, PACK, P], F32, name="h_acc%d" % i, tag="bank%d" % (4 + i)) for i in range(PACK)]
-        for g in range(PASSES - 1):
+        for g in range(PASSES - 2):
             grouped = cast_and_deal(d_raw[g], SCALAR_SHARE)
             quantize(d_codes[g], d_plane[g], grouped, 0, R)
             for i in range(PACK):
                 for j in range(PACK):
                     h_pass(g, i, j)
+        g = PASSES - 2
+        grouped = cast_and_deal(d_raw[g], SCALAR_SHARE)
+        for j in range(PACK):
+            quantize(d_codes[g], d_plane[g], grouped[:, cols(j, K_PASS)], j * P, P)
+            for i in range(PACK):
+                h_pass(g, i, j)
         g = PASSES - 1
         grouped = cast_and_deal(d_raw[g], LAST_SHARE)
         for half in range(2):

@@ -25,6 +25,7 @@ QUARTER = 256
 SCALAR_SHARE = 48
 PARK_SHARE = 64
 LAST_SHARE = 42
+SECOND_SHARE = 80
 
 
 def tile_mix_three_tm_pl_bias_kernel(
@@ -50,7 +51,7 @@ def tile_mix_three_tm_pl_bias_kernel(
         w8_high = kept("w8_high", [P, PASSES8, HALF], U32)
         w4_codes = kept("w4_codes", [P, PASSES4, 2 * M], U8)
         up_codes = kept("up_codes", [P, 2 * M], U8)
-        w8_plane = [kept("w8_plane%d" % h, [P, PASSES8, HALF], U8) for h in range(2)]
+        w8_plane = kept("w8_plane", [P, PASSES8, M], U8)
         w4_plane = kept("w4_plane", [P, PASSES4, M], U8)
         up_plane = kept("up_plane", [P, 1, M], U8)
         ident = kept("ident", [P, P], F32)
@@ -120,7 +121,7 @@ def tile_mix_three_tm_pl_bias_kernel(
                 lhsT=x_codes[g][:, cols(i, P)].bitcast(FP8X4),
                 lhsT_scale=x_plane[g][:, cols(i, P)],
                 rhs=words.bitcast(FP8X4),
-                rhs_scale=w8_plane[first // HALF][:, g, first % HALF : first % HALF + width],
+                rhs_scale=w8_plane[:, g, first : first + width],
                 start=start,
                 stop=False,
             )
@@ -143,8 +144,8 @@ def tile_mix_three_tm_pl_bias_kernel(
                 lhsT_scale=d_plane[g][:, cols(j, P)],
                 rhs=x_codes[g][:, cols(i, P)].bitcast(FP8X4),
                 rhs_scale=x_plane[g][:, cols(i, P)],
-                start=(g == 0 and j == 0),
-                stop=(g == PASSES - 1 and j == PACK - 1),
+                start=(g == PASSES8 and j == 0),
+                stop=(g == 1 and j == PACK - 1),
             )
 
         def add(out, acc, other):
@@ -160,7 +161,7 @@ def tile_mix_three_tm_pl_bias_kernel(
 
         nc.scalar.dma_start(out=b_cols[:], in_=b.rearrange("(p c) -> p c", p=P))
         make_identity(nc, ident[:])
-        for plane in (w4_plane, w8_plane[0], up_plane, w8_plane[1]):
+        for plane in (w4_plane, w8_plane, up_plane):
             nc.vector.memset(plane[:].bitcast(I32), 0)
 
         load_rows(x_raw, x, 2)
@@ -168,17 +169,19 @@ def tile_mix_three_tm_pl_bias_kernel(
         load_plane(w4_plane, w4_scales)
         load_rows(x_raw, x, 3)
         load_rows(x_raw, x, 4)
-        load_plane(w8_plane[0], w8_scales, cols(0, HALF))
         load_rows(x_raw, x, 0)
+        load_rows(d_raw, down, 1)
+        load_rows(d_raw, down, 2)
+        load_rows(d_raw, down, 3)
+        load_rows(d_raw, down, 4)
+        load_rows(d_raw, down, 0)
         load_rows(x_raw, x, 1)
-        for g in range(PASSES):
-            load_rows(d_raw, down, g)
+        load_plane(w8_plane, w8_scales)
         nc.sync.dma_start(out=w8_low[0][:].bitcast(I32), in_=w8_view[:, 0, cols(0, PACK * HALF)].bitcast(I32))
-        load_plane(up_plane, up_scales)
         nc.sync.dma_start(out=w8_low[1][:].bitcast(I32), in_=w8_view[:, 1, cols(0, PACK * HALF)].bitcast(I32))
         nc.sync.dma_start(out=up_codes[:].bitcast(I32), in_=up_words[0].bitcast(I32))
+        load_plane(up_plane, up_scales)
         nc.sync.dma_start(out=w8_high[:].bitcast(I32), in_=w8_view[:, :, cols(1, PACK * HALF)].bitcast(I32))
-        load_plane(w8_plane[1], w8_scales, cols(1, HALF))
 
         spread = [psum.tile([P, PACK, P], F32, name="spread%d" % h, tag="bank%d" % (4 + h)) for h in range(2)]
         for h in range(2):
@@ -202,36 +205,43 @@ def tile_mix_three_tm_pl_bias_kernel(
             for i in range(PACK):
                 w4_pass(y_low[i], g, i, 0, g == PASSES8, False)
 
-        for g in range(PASSES8):
-            grouped = cast_and_deal(x_raw[g], PARK_SHARE)
-            for i in (2 * g, 2 * g + 1):
+        for n, (raw, codes, plane) in enumerate(((x_raw[0], x_codes[0], x_plane[0]), (d_raw[1], d_codes[1], d_plane[1]))):
+            grouped = cast_and_deal(raw, PARK_SHARE)
+            for i in (2 * n, 2 * n + 1):
                 add(parked[:, i, :], y_early[i][:], bias[:, cols(1, HALF)])
-            quantize(x_codes[g], x_plane[g], grouped, 0, T)
+            quantize(codes, plane, grouped, 0, T)
 
         h_acc = [psum.tile([P, PACK, P], F32, name="h_acc%d" % i, tag="bank%d" % (4 + i)) for i in range(PACK)]
-        for g in range(PASSES - 2):
+        for g in range(PASSES8, PASSES):
             grouped = cast_and_deal(d_raw[g], SCALAR_SHARE)
             quantize(d_codes[g], d_plane[g], grouped, 0, R)
             for i in range(PACK):
                 for j in range(PACK):
                     h_pass(g, i, j)
-        g = PASSES - 2
-        grouped = cast_and_deal(d_raw[g], SCALAR_SHARE)
+        grouped = cast_and_deal(d_raw[0], SCALAR_SHARE)
         for j in range(PACK):
-            quantize(d_codes[g], d_plane[g], grouped[:, cols(j, K_PASS)], j * P, P)
+            quantize(d_codes[0], d_plane[0], grouped[:, cols(j, K_PASS)], j * P, P)
             for i in range(PACK):
-                h_pass(g, i, j)
-        g = PASSES - 1
-        grouped = cast_and_deal(d_raw[g], LAST_SHARE)
-        for half in range(2):
-            quantize(d_codes[g], d_plane[g], grouped[:, cols(half, 2 * K_PASS)], half * 2 * P, 2 * P)
-        for i in range(PACK):
-            w8_pass(y_low[i][:], 0, i, w8_low[0][:], 0, HALF, False)
-        for i, j in ((0, 0), (0, 1), (1, 0), (1, 1), (0, 2), (0, 3), (1, 2), (1, 3)):
-            h_pass(g, i, j)
-        for i in (2, 3):
+                h_pass(0, i, j)
+        last = kept("last_grouped", [P, PACK, P, PACK], BF16)
+        last_dst = last[:].rearrange("p i m j -> p m j i")
+        last_src = x_raw[1][:].rearrange("p j (m i) -> p m j i", i=PACK)
+
+        def cast_slots(copy, ms, pair):
+            copy(out=last_dst[:, ms, :, cols(pair, 2)], in_=last_src[:, ms, :, cols(pair, 2)])
+
+        def quantize_slot(i):
+            quantize(x_codes[1], x_plane[1], last[:, i].rearrange("p m j -> p (m j)"), i * P, P)
+
+        def low_w8(i, g):
+            w8_pass(y_low[i][:], g, i, w8_low[g][:], 0, HALF, False)
+
+        def low_up(i):
+            up_pass(y_low[i][:], i, 0, HALF, True)
+
+        def h_close(i):
             for j in range(PACK):
-                h_pass(g, i, j)
+                h_pass(1, i, j)
 
         def h_out(copy, i):
             copy(out=h_grouped[i][:], in_=h_acc[i][:].rearrange("p j t -> p t j"))
@@ -245,69 +255,94 @@ def tile_mix_three_tm_pl_bias_kernel(
             if first + width == HALF:
                 nc.sync.dma_start(out=out_rows[:, i, cols(0, HALF)], in_=result[0][:, i, :])
 
-        h_out(nc.scalar.copy, 0)
-        h_out(nc.vector.tensor_copy, 1)
-        h_out(nc.scalar.copy, 2)
-        h_out(nc.scalar.copy, 3)
-        for i in range(3):
-            h_quantize(i)
+        def high_tile(bank, n, width):
+            return psum.tile([P, n, width], F32, name="y_high%d" % bank, tag="bank%d" % bank)
 
-        def low_w8(i, g):
-            w8_pass(y_low[i][:], g, i, w8_low[g][:], 0, HALF, False)
-
-        def low_up(i):
-            up_pass(y_low[i][:], i, 0, HALF, True)
-
-        low_w8(0, 1)
-        low_w8(1, 1)
-        low_up(0)
-        low_up(1)
-        add_low(0, 0, HALF)
-        h_quantize(3)
-        for i in (2, 3):
-            low_w8(i, 1)
-            low_up(i)
-        add_low(1, 0, HALF)
-        add_low(2, 0, HALF)
-        add_low(3, 0, QUARTER)
-        interleave(nc.scalar.copy, 0, 0, QUARTER)
-        add_low(3, QUARTER, QUARTER)
-        interleave(nc.scalar.copy, 0, QUARTER, QUARTER)
-
-        def high_bank(bank, slots, first, width):
-            n = len(slots)
-            acc = psum.tile([P, n, width], F32, name="y_high", tag="bank%d" % bank)
-            c = slice(first, first + width)
-            rows = slice(slots[0], slots[0] + n)
+        def high_w8(acc, slots, first, width):
             for g in range(PASSES8):
                 for e, i in enumerate(slots):
-                    w8_pass(acc[:, e, :], g, i, w8_high[:, g, c], HALF + first, width, g == 0 and e == 0)
+                    w8_pass(acc[:, e, :], g, i, w8_high[:, g, first : first + width], HALF + first, width, g == 0 and e == 0)
+
+        def high_up(acc, slots, first, width):
             step = HALF if width == HALF else P
             for e, i in enumerate(slots):
                 for u in range(0, width, step):
-                    up_pass(acc[:, e, u : u + step], i, HALF + first + u, step, e == n - 1 and u + step == width)
+                    up_pass(acc[:, e, u : u + step], i, HALF + first + u, step, e == len(slots) - 1 and u + step == width)
+
+        def add_high(acc, slots, first, width):
+            rows, c = slice(slots[0], slots[-1] + 1), slice(first, first + width)
             add(result[1][:, rows, c], acc[:], parked[:, rows, c])
+
+        def high_bank(bank, slots, first, width):
+            acc = high_tile(bank, len(slots), width)
+            high_w8(acc, slots, first, width)
+            high_up(acc, slots, first, width)
+            return acc
 
         def store_high(rows, first, width):
             nc.sync.dma_start(
                 out=out_rows[:, rows, HALF + first : HALF + first + width], in_=result[1][:, rows, first : first + width]
             )
 
+        S, V = nc.scalar.copy, nc.vector.tensor_copy
+        cast_slots(S, slice(0, LAST_SHARE), 0)
+        cast_slots(V, slice(LAST_SHARE, P), 0)
+        cast_slots(S, slice(0, SECOND_SHARE), 1)
+        quantize_slot(0)
+        quantize_slot(1)
+        cast_slots(V, slice(SECOND_SHARE, P), 1)
+        low_w8(0, 0)
+        h_close(0)
+        h_close(1)
+        low_w8(1, 0)
+        h_out(S, 0)
+        quantize_slot(2)
+        quantize_slot(3)
+        h_out(V, 1)
+        h_close(2)
+        low_w8(0, 1)
+        h_out(S, 2)
+        h_close(3)
+        h_quantize(0)
+        h_quantize(1)
+        low_up(0)
+        low_w8(1, 1)
+        low_up(1)
+        h_out(S, 3)
+        add_low(0, 0, HALF)
+        h_quantize(2)
+        low_w8(2, 0)
+        low_w8(2, 1)
+        low_up(2)
+        add_low(1, 0, HALF)
+        h_quantize(3)
+        low_w8(3, 0)
+        low_w8(3, 1)
+        low_up(3)
+        add_low(2, 0, HALF)
+        add_low(3, 0, QUARTER)
+        interleave(S, 0, 0, QUARTER)
+        add_low(3, QUARTER, QUARTER)
+        interleave(S, 0, QUARTER, QUARTER)
         for i in range(2):
-            high_bank(4 + i, (i,), 0, HALF)
+            acc = high_bank(4 + i, (i,), 0, HALF)
+            add_high(acc, (i,), 0, HALF)
             store_high(slice(i, i + 1), 0, HALF)
         quantize_out(0, 0, QUARTER)
-        high_bank(6, (2, 3), 0, QUARTER)
+        acc = high_bank(6, (2, 3), 0, QUARTER)
+        add_high(acc, (2, 3), 0, QUARTER)
         store_high(slice(2, 4), 0, QUARTER)
-        interleave(nc.scalar.copy, 1, 0, P)
-        high_bank(7, (2, 3), QUARTER, P)
-        interleave(nc.scalar.copy, 1, QUARTER, P)
+        interleave(S, 1, 0, P)
+        acc = high_bank(7, (2, 3), QUARTER, P)
+        add_high(acc, (2, 3), QUARTER, P)
+        interleave(S, 1, QUARTER, P)
         quantize_out(0, QUARTER, QUARTER)
         store_words(0, HALF)
-        high_bank(0, (2, 3), QUARTER + P, P)
+        acc = high_bank(0, (2, 3), QUARTER + P, P)
+        add_high(acc, (2, 3), QUARTER + P, P)
         store_high(slice(2, 4), QUARTER, QUARTER)
-        interleave(nc.vector.tensor_copy, 1, P, P)
-        interleave(nc.vector.tensor_copy, 1, QUARTER + P, P)
+        interleave(V, 1, P, P)
+        interleave(V, 1, QUARTER + P, P)
         quantize_out(1, 0, QUARTER)
         store_words(HALF, QUARTER)
         quantize_out(1, QUARTER, QUARTER)

@@ -25,7 +25,6 @@ QUARTER = 256
 SCALAR_SHARE = 48
 PARK_SHARE = 64
 LAST_SHARE = 42
-SECOND_SHARE = 80
 
 
 def tile_mix_three_tm_pl_bias_kernel(
@@ -227,9 +226,6 @@ def tile_mix_three_tm_pl_bias_kernel(
         last_dst = last[:].rearrange("p i m j -> p m j i")
         last_src = x_raw[1][:].rearrange("p j (m i) -> p m j i", i=PACK)
 
-        def cast_slots(copy, ms, pair):
-            copy(out=last_dst[:, ms, :, cols(pair, 2)], in_=last_src[:, ms, :, cols(pair, 2)])
-
         def quantize_slot(i):
             quantize(x_codes[1], x_plane[1], last[:, i].rearrange("p m j -> p (m j)"), i * P, P)
 
@@ -285,37 +281,33 @@ def tile_mix_three_tm_pl_bias_kernel(
             )
 
         S, V = nc.scalar.copy, nc.vector.tensor_copy
-        cast_slots(S, slice(0, LAST_SHARE), 0)
-        cast_slots(V, slice(LAST_SHARE, P), 0)
-        cast_slots(S, slice(0, SECOND_SHARE), 1)
-        quantize_slot(0)
-        quantize_slot(1)
-        cast_slots(V, slice(SECOND_SHARE, P), 1)
+        nc.scalar.copy(out=last_dst[:, :LAST_SHARE], in_=last_src[:, :LAST_SHARE])
+        nc.vector.tensor_copy(out=last_dst[:, LAST_SHARE:], in_=last_src[:, LAST_SHARE:])
+        for i in range(PACK):
+            quantize_slot(i)
         low_w8(0, 0)
         h_close(0)
         h_close(1)
-        low_w8(1, 0)
         h_out(S, 0)
-        quantize_slot(2)
-        quantize_slot(3)
         h_out(V, 1)
         h_close(2)
-        low_w8(0, 1)
         h_out(S, 2)
         h_close(3)
+        low_w8(0, 1)
+        low_w8(1, 0)
         h_quantize(0)
         h_quantize(1)
         low_up(0)
         low_w8(1, 1)
         low_up(1)
         h_out(S, 3)
-        add_low(0, 0, HALF)
         h_quantize(2)
+        add_low(0, 0, HALF)
         low_w8(2, 0)
         low_w8(2, 1)
         low_up(2)
-        add_low(1, 0, HALF)
         h_quantize(3)
+        add_low(1, 0, HALF)
         low_w8(3, 0)
         low_w8(3, 1)
         low_up(3)

@@ -50,7 +50,7 @@ def tile_mix_three_tm_pl_bias_kernel(
         w8_high = kept("w8_high", [P, PASSES8, HALF], U32)
         w4_codes = kept("w4_codes", [P, PASSES4, 2 * M], U8)
         up_codes = kept("up_codes", [P, 2 * M], U8)
-        w8_plane = kept("w8_plane", [P, PASSES8, M], U8)
+        w8_plane = [kept("w8_plane%d" % h, [P, PASSES8, HALF], U8) for h in range(2)]
         w4_plane = kept("w4_plane", [P, PASSES4, M], U8)
         up_plane = kept("up_plane", [P, 1, M], U8)
         ident = kept("ident", [P, P], F32)
@@ -120,7 +120,7 @@ def tile_mix_three_tm_pl_bias_kernel(
                 lhsT=x_codes[g][:, cols(i, P)].bitcast(FP8X4),
                 lhsT_scale=x_plane[g][:, cols(i, P)],
                 rhs=words.bitcast(FP8X4),
-                rhs_scale=w8_plane[:, g, first : first + width],
+                rhs_scale=w8_plane[first // HALF][:, g, first % HALF : first % HALF + width],
                 start=start,
                 stop=False,
             )
@@ -160,7 +160,7 @@ def tile_mix_three_tm_pl_bias_kernel(
 
         nc.scalar.dma_start(out=b_cols[:], in_=b.rearrange("(p c) -> p c", p=P))
         make_identity(nc, ident[:])
-        for plane in (w4_plane, w8_plane, up_plane):
+        for plane in (w4_plane, w8_plane[0], up_plane, w8_plane[1]):
             nc.vector.memset(plane[:].bitcast(I32), 0)
 
         load_rows(x_raw, x, 2)
@@ -168,6 +168,7 @@ def tile_mix_three_tm_pl_bias_kernel(
         load_plane(w4_plane, w4_scales)
         load_rows(x_raw, x, 3)
         load_rows(x_raw, x, 4)
+        load_plane(w8_plane[0], w8_scales, cols(0, HALF))
         load_rows(x_raw, x, 0)
         load_rows(d_raw, down, 1)
         load_rows(d_raw, down, 2)
@@ -175,12 +176,12 @@ def tile_mix_three_tm_pl_bias_kernel(
         load_rows(d_raw, down, 4)
         load_rows(d_raw, down, 0)
         load_rows(x_raw, x, 1)
-        load_plane(w8_plane, w8_scales)
         nc.sync.dma_start(out=w8_low[0][:].bitcast(I32), in_=w8_view[:, 0, cols(0, PACK * HALF)].bitcast(I32))
+        load_plane(up_plane, up_scales)
         nc.sync.dma_start(out=w8_low[1][:].bitcast(I32), in_=w8_view[:, 1, cols(0, PACK * HALF)].bitcast(I32))
         nc.sync.dma_start(out=up_codes[:].bitcast(I32), in_=up_words[0].bitcast(I32))
-        load_plane(up_plane, up_scales)
         nc.sync.dma_start(out=w8_high[:].bitcast(I32), in_=w8_view[:, :, cols(1, PACK * HALF)].bitcast(I32))
+        load_plane(w8_plane[1], w8_scales, cols(1, HALF))
 
         spread = [psum.tile([P, PACK, P], F32, name="spread%d" % h, tag="bank%d" % (4 + h)) for h in range(2)]
         for h in range(2):
@@ -285,7 +286,8 @@ def tile_mix_three_tm_pl_bias_kernel(
         nc.vector.tensor_copy(out=last_dst[:, LAST_SHARE:], in_=last_src[:, LAST_SHARE:])
         for i in range(PACK):
             quantize_slot(i)
-        low_w8(0, 0)
+        for i in range(3):
+            low_w8(i, 0)
         h_close(0)
         h_close(1)
         h_out(S, 0)
@@ -294,16 +296,14 @@ def tile_mix_three_tm_pl_bias_kernel(
         h_out(S, 2)
         h_close(3)
         low_w8(0, 1)
-        low_w8(1, 0)
+        low_w8(1, 1)
         h_quantize(0)
         h_quantize(1)
         low_up(0)
-        low_w8(1, 1)
         low_up(1)
         h_out(S, 3)
         h_quantize(2)
         add_low(0, 0, HALF)
-        low_w8(2, 0)
         low_w8(2, 1)
         low_up(2)
         h_quantize(3)

@@ -22,9 +22,11 @@ PASSES8 = O // K_PASS
 PASSES4 = PASSES - PASSES8
 HALF = 512
 QUARTER = 256
+W8_ROW = 4
 SCALAR_SHARE = 48
 PARK_SHARE = 64
 LAST_SHARE = 42
+SECOND_SHARE = 80
 
 
 def tile_mix_three_tm_pl_bias_kernel(
@@ -73,10 +75,10 @@ def tile_mix_three_tm_pl_bias_kernel(
 
         w8_view = w8_words.rearrange("a p n i -> p a (n i)")
 
-        def load_plane(plane, scales, n_cols=slice(0, M)):
+        def load_plane(plane, scales, n_cols=slice(0, M), row=0):
             rows = scales.rearrange("a (q r) n -> r q a n", r=4)
             for r in range(4):
-                nc.sync.dma_start(out=plane[:].bitcast(I32)[r:P:32], in_=rows[r][:, :, n_cols].bitcast(I32))
+                nc.sync.dma_start(out=plane[:].bitcast(I32)[row + r : P : 32], in_=rows[r][:, :, n_cols].bitcast(I32))
 
         def cast_and_deal(raw, share):
             grouped = stage.tile([P, PACK, P, PACK], BF16, name="grouped", align_bytes=64)
@@ -120,7 +122,7 @@ def tile_mix_three_tm_pl_bias_kernel(
                 lhsT=x_codes[g][:, cols(i, P)].bitcast(FP8X4),
                 lhsT_scale=x_plane[g][:, cols(i, P)],
                 rhs=words.bitcast(FP8X4),
-                rhs_scale=w8_plane[first // HALF][:, g, first % HALF : first % HALF + width],
+                rhs_scale=w8_plane[first // HALF][W8_ROW:, g, first % HALF : first % HALF + width],
                 start=start,
                 stop=False,
             )
@@ -168,7 +170,7 @@ def tile_mix_three_tm_pl_bias_kernel(
         load_plane(w4_plane, w4_scales)
         load_rows(x_raw, x, 3)
         load_rows(x_raw, x, 4)
-        load_plane(w8_plane[0], w8_scales, cols(0, HALF))
+        load_plane(w8_plane[0], w8_scales, cols(0, HALF), W8_ROW)
         load_rows(x_raw, x, 0)
         load_rows(d_raw, down, 1)
         load_rows(d_raw, down, 2)
@@ -181,7 +183,7 @@ def tile_mix_three_tm_pl_bias_kernel(
         nc.sync.dma_start(out=w8_low[1][:].bitcast(I32), in_=w8_view[:, 1, cols(0, PACK * HALF)].bitcast(I32))
         nc.sync.dma_start(out=up_codes[:].bitcast(I32), in_=up_words[0].bitcast(I32))
         nc.sync.dma_start(out=w8_high[:].bitcast(I32), in_=w8_view[:, :, cols(1, PACK * HALF)].bitcast(I32))
-        load_plane(w8_plane[1], w8_scales, cols(1, HALF))
+        load_plane(w8_plane[1], w8_scales, cols(1, HALF), W8_ROW)
 
         spread = [psum.tile([P, PACK, P], F32, name="spread%d" % h, tag="bank%d" % (4 + h)) for h in range(2)]
         for h in range(2):
@@ -218,7 +220,7 @@ def tile_mix_three_tm_pl_bias_kernel(
             for i in range(PACK):
                 for j in range(PACK):
                     h_pass(g, i, j)
-        grouped = cast_and_deal(d_raw[0], SCALAR_SHARE)
+        grouped = cast_and_deal(d_raw[0], LAST_SHARE)
         for j in range(PACK):
             quantize(d_codes[0], d_plane[0], grouped[:, cols(j, K_PASS)], j * P, P)
             for i in range(PACK):
@@ -226,6 +228,9 @@ def tile_mix_three_tm_pl_bias_kernel(
         last = kept("last_grouped", [P, PACK, P, PACK], BF16)
         last_dst = last[:].rearrange("p i m j -> p m j i")
         last_src = x_raw[1][:].rearrange("p j (m i) -> p m j i", i=PACK)
+
+        def cast_slots(copy, ms, pair):
+            copy(out=last_dst[:, ms, :, cols(pair, 2)], in_=last_src[:, ms, :, cols(pair, 2)])
 
         def quantize_slot(i):
             quantize(x_codes[1], x_plane[1], last[:, i].rearrange("p m j -> p (m j)"), i * P, P)
@@ -241,7 +246,10 @@ def tile_mix_three_tm_pl_bias_kernel(
                 h_pass(1, i, j)
 
         def h_out(copy, i):
-            copy(out=h_grouped[i][:], in_=h_acc[i][:].rearrange("p j t -> p t j"))
+            copy(
+                out=h_grouped[i][:].rearrange("p (c u) j -> p c j u", u=4),
+                in_=h_acc[i][:].rearrange("p j (c u) -> p c j u", u=4),
+            )
 
         def h_quantize(i):
             quantize(h_codes, h_plane, h_grouped[i][:].rearrange("p t j -> p (t j)"), i * P, P)
@@ -282,28 +290,33 @@ def tile_mix_three_tm_pl_bias_kernel(
             )
 
         S, V = nc.scalar.copy, nc.vector.tensor_copy
-        nc.scalar.copy(out=last_dst[:, :LAST_SHARE], in_=last_src[:, :LAST_SHARE])
-        nc.vector.tensor_copy(out=last_dst[:, LAST_SHARE:], in_=last_src[:, LAST_SHARE:])
-        for i in range(PACK):
-            quantize_slot(i)
-        for i in range(3):
-            low_w8(i, 0)
+        cast_slots(S, slice(0, LAST_SHARE), 0)
+        cast_slots(V, slice(LAST_SHARE, P), 0)
+        cast_slots(S, slice(0, SECOND_SHARE), 1)
+        quantize_slot(0)
+        quantize_slot(1)
+        cast_slots(V, slice(SECOND_SHARE, P), 1)
+        low_w8(0, 0)
+        low_w8(1, 0)
         h_close(0)
         h_close(1)
         h_out(S, 0)
+        quantize_slot(2)
+        quantize_slot(3)
         h_out(V, 1)
+        low_w8(0, 1)
         h_close(2)
         h_out(S, 2)
         h_close(3)
-        low_w8(0, 1)
-        low_w8(1, 1)
         h_quantize(0)
         h_quantize(1)
+        low_w8(1, 1)
         low_up(0)
         low_up(1)
         h_out(S, 3)
         h_quantize(2)
         add_low(0, 0, HALF)
+        low_w8(2, 0)
         low_w8(2, 1)
         low_up(2)
         h_quantize(3)

@@ -50,7 +50,9 @@ def tile_mix_three_tm_pl_bias_kernel(
         d_plane = [kept("d_plane%d" % g, [P, R], U8) for g in range(PASSES)]
         w8_low = [kept("w8_low%d" % g, [P, HALF], U32) for g in range(PASSES8)]
         w8_high = kept("w8_high", [P, PASSES8, HALF], U32)
-        w4_codes = kept("w4_codes", [P, PASSES4, 2 * M], U8)
+        w4_first = kept("w4_first", [P, PASSES4 - 1, 2 * M], U8)
+        w4_last = kept("w4_last", [P, 2 * M], U8)
+        w4_codes = [w4_first[:, 0, :], w4_first[:, 1, :], w4_last[:]]
         up_codes = kept("up_codes", [P, 2 * M], U8)
         w8_plane = [kept("w8_plane%d" % h, [P, PASSES8, HALF], U8) for h in range(2)]
         w4_plane = kept("w4_plane", [P, PASSES4, M], U8)
@@ -70,8 +72,8 @@ def tile_mix_three_tm_pl_bias_kernel(
         def cols(n, width):
             return slice(n * width, (n + 1) * width)
 
-        def load_rows(raw, src, g):
-            nc.sync.dma_start(out=raw[g][:], in_=src[cols(g, K_PASS), :].rearrange("(p j) w -> p j w", j=PACK))
+        def load_rows(raw, src, g, queue=nc.sync):
+            queue.dma_start(out=raw[g][:], in_=src[cols(g, K_PASS), :].rearrange("(p j) w -> p j w", j=PACK))
 
         w8_view = w8_words.rearrange("a p n i -> p a (n i)")
 
@@ -110,7 +112,7 @@ def tile_mix_three_tm_pl_bias_kernel(
                 out=acc[:],
                 lhsT=x_codes[g][:, cols(i, P)].bitcast(FP8X4),
                 lhsT_scale=x_plane[g][:, cols(i, P)],
-                rhs=w4_codes[:, g - PASSES8, cols(h, 2 * HALF)].bitcast(FP4X4),
+                rhs=w4_codes[g - PASSES8][:, cols(h, 2 * HALF)].bitcast(FP4X4),
                 rhs_scale=w4_plane[:, g - PASSES8, cols(h, HALF)],
                 start=start,
                 stop=stop,
@@ -166,24 +168,26 @@ def tile_mix_three_tm_pl_bias_kernel(
             nc.vector.memset(plane[:].bitcast(I32), 0)
 
         load_rows(x_raw, x, 2)
-        nc.sync.dma_start(out=w4_codes[:].bitcast(I32), in_=w4_words.rearrange("a p c -> p a c").bitcast(I32))
+        w4_rows = w4_words.rearrange("a p c -> p a c")
+        nc.scalar.dma_start(out=w4_first[:].bitcast(I32), in_=w4_rows[:, : PASSES4 - 1, :].bitcast(I32))
+        load_rows(x_raw, x, 3, nc.scalar)
         load_plane(w4_plane, w4_scales)
-        load_rows(x_raw, x, 3)
         load_rows(x_raw, x, 4)
+        nc.sync.dma_start(out=w4_last[:].bitcast(I32), in_=w4_words[PASSES4 - 1].bitcast(I32))
+        load_rows(x_raw, x, 0, nc.scalar)
         load_plane(w8_plane[0], w8_scales, cols(0, HALF), W8_ROW)
-        load_rows(x_raw, x, 0)
         load_rows(d_raw, down, 1)
-        load_rows(d_raw, down, 2)
-        load_rows(d_raw, down, 3)
-        load_rows(d_raw, down, 4)
-        load_rows(d_raw, down, 0)
-        load_rows(x_raw, x, 1)
-        nc.sync.dma_start(out=w8_low[0][:].bitcast(I32), in_=w8_view[:, 0, cols(0, PACK * HALF)].bitcast(I32))
-        load_plane(up_plane, up_scales)
-        nc.sync.dma_start(out=w8_low[1][:].bitcast(I32), in_=w8_view[:, 1, cols(0, PACK * HALF)].bitcast(I32))
-        nc.sync.dma_start(out=up_codes[:].bitcast(I32), in_=up_words[0].bitcast(I32))
-        nc.sync.dma_start(out=w8_high[:].bitcast(I32), in_=w8_view[:, :, cols(1, PACK * HALF)].bitcast(I32))
-        load_plane(w8_plane[1], w8_scales, cols(1, HALF), W8_ROW)
+
+        def load_the_rest():
+            load_rows(d_raw, down, 4, nc.scalar)
+            load_rows(d_raw, down, 0)
+            load_rows(x_raw, x, 1)
+            nc.sync.dma_start(out=w8_low[0][:].bitcast(I32), in_=w8_view[:, 0, cols(0, PACK * HALF)].bitcast(I32))
+            load_plane(up_plane, up_scales)
+            nc.sync.dma_start(out=w8_low[1][:].bitcast(I32), in_=w8_view[:, 1, cols(0, PACK * HALF)].bitcast(I32))
+            nc.sync.dma_start(out=up_codes[:].bitcast(I32), in_=up_words[0].bitcast(I32))
+            nc.sync.dma_start(out=w8_high[:].bitcast(I32), in_=w8_view[:, :, cols(1, PACK * HALF)].bitcast(I32))
+            load_plane(w8_plane[1], w8_scales, cols(1, HALF), W8_ROW)
 
         spread = [psum.tile([P, PACK, P], F32, name="spread%d" % h, tag="bank%d" % (4 + h)) for h in range(2)]
         for h in range(2):
@@ -193,6 +197,9 @@ def tile_mix_three_tm_pl_bias_kernel(
         y_low = [psum.tile([P, HALF], F32, name="y_low%d" % i, tag="bank%d" % i) for i in range(PACK)]
         y_early = []
         for g in range(PASSES8, PASSES):
+            if g == PASSES - 1:
+                load_rows(d_raw, down, 2, nc.scalar)
+                load_rows(d_raw, down, 3)
             grouped = cast_and_deal(x_raw[g], SCALAR_SHARE)
             quantize(x_codes[g], x_plane[g], grouped, 0, T)
             if g == PASSES8:
@@ -207,6 +214,7 @@ def tile_mix_three_tm_pl_bias_kernel(
             for i in range(PACK):
                 w4_pass(y_low[i], g, i, 0, g == PASSES8, False)
 
+        load_the_rest()
         for n, (raw, codes, plane) in enumerate(((x_raw[0], x_codes[0], x_plane[0]), (d_raw[1], d_codes[1], d_plane[1]))):
             grouped = cast_and_deal(raw, PARK_SHARE)
             for i in (2 * n, 2 * n + 1):

@@ -27,6 +27,7 @@ SCALAR_SHARE = 48
 PARK_SHARE = 64
 LAST_SHARE = 42
 SECOND_SHARE = 80
+HIGH_SHARE = 160
 
 
 def tile_mix_three_tm_pl_bias_kernel(
@@ -297,6 +298,11 @@ def tile_mix_three_tm_pl_bias_kernel(
                 out=out_rows[:, rows, HALF + first : HALF + first + width], in_=result[1][:, rows, first : first + width]
             )
 
+        def G(out, in_):
+            nc.gpsimd.tensor_scalar(
+                out=out, in0=in_, scalar1=1.0, scalar2=0.0, op0=mybir.AluOpType.mult, op1=mybir.AluOpType.add
+            )
+
         S, V = nc.scalar.copy, nc.vector.tensor_copy
         cast_slots(S, slice(0, LAST_SHARE), 0)
         cast_slots(V, slice(LAST_SHARE, P), 0)
@@ -336,7 +342,8 @@ def tile_mix_three_tm_pl_bias_kernel(
         add_low(3, 0, QUARTER)
         interleave(S, 0, 0, QUARTER)
         add_low(3, QUARTER, QUARTER)
-        interleave(S, 0, QUARTER, QUARTER)
+        interleave(G, 0, QUARTER + P, P)
+        interleave(S, 0, QUARTER, P)
         for i in range(2):
             acc = high_bank(4 + i, (i,), 0, HALF)
             add_high(acc, (i,), 0, HALF)
@@ -345,16 +352,16 @@ def tile_mix_three_tm_pl_bias_kernel(
         acc = high_bank(6, (2, 3), 0, QUARTER)
         add_high(acc, (2, 3), 0, QUARTER)
         store_high(slice(2, 4), 0, QUARTER)
-        interleave(S, 1, 0, P)
+        interleave(S, 1, 0, HIGH_SHARE)
+        quantize_out(0, QUARTER, QUARTER)
+        store_words(0, HALF)
         acc = high_bank(7, (2, 3), QUARTER, P)
         add_high(acc, (2, 3), QUARTER, P)
         interleave(S, 1, QUARTER, P)
-        quantize_out(0, QUARTER, QUARTER)
-        store_words(0, HALF)
         acc = high_bank(0, (2, 3), QUARTER + P, P)
         add_high(acc, (2, 3), QUARTER + P, P)
         store_high(slice(2, 4), QUARTER, QUARTER)
-        interleave(V, 1, P, P)
+        interleave(V, 1, HIGH_SHARE, QUARTER - HIGH_SHARE)
         interleave(V, 1, QUARTER + P, P)
         quantize_out(1, 0, QUARTER)
         store_words(HALF, QUARTER)

@@ -349,23 +349,24 @@ def tile_mix_three_tm_pl_bias_kernel(
             add_high(acc, (i,), 0, HALF)
             store_high(slice(i, i + 1), 0, HALF)
         quantize_out(0, 0, QUARTER)
+        store_words(0, QUARTER)
         acc = high_bank(6, (2, 3), 0, QUARTER)
         add_high(acc, (2, 3), 0, QUARTER)
         store_high(slice(2, 4), 0, QUARTER)
         interleave(S, 1, 0, HIGH_SHARE)
-        quantize_out(0, QUARTER, QUARTER)
-        store_words(0, HALF)
         acc = high_bank(7, (2, 3), QUARTER, P)
         add_high(acc, (2, 3), QUARTER, P)
         interleave(S, 1, QUARTER, P)
+        interleave(V, 1, HIGH_SHARE, QUARTER - HIGH_SHARE)
         acc = high_bank(0, (2, 3), QUARTER + P, P)
         add_high(acc, (2, 3), QUARTER + P, P)
         store_high(slice(2, 4), QUARTER, QUARTER)
-        interleave(V, 1, HIGH_SHARE, QUARTER - HIGH_SHARE)
-        interleave(V, 1, QUARTER + P, P)
+        quantize_out(0, QUARTER, QUARTER)
         quantize_out(1, 0, QUARTER)
-        store_words(HALF, QUARTER)
-        quantize_out(1, QUARTER, QUARTER)
+        store_words(QUARTER, HALF)
+        interleave(V, 1, QUARTER + P, P)
+        quantize_out(1, QUARTER, P)
+        quantize_out(1, QUARTER + P, P)
         store_words(HALF + QUARTER, QUARTER)
         for q in range(4):
             queue = nc.sync if q < 2 else nc.scalar

from contextlib import ExitStack

import concourse.mybir as mybir
from concourse.masks import make_identity

O, K, R, M, T = 1024, 2560, 512, 1024, 512
FLOPS = 2 * T * (K * M + K * R + R * M)

F32 = mybir.dt.float32
BF16 = mybir.dt.bfloat16
I32 = mybir.dt.int32
U32 = mybir.dt.uint32
U8 = mybir.dt.uint8
FP8X4 = mybir.dt.float8_e4m3fn_x4
FP4X4 = mybir.dt.float4_e2m1fn_x4

P = 128
PACK = 4
K_PASS = P * PACK
PASSES = K // K_PASS
PASSES8 = O // K_PASS
PASSES4 = PASSES - PASSES8
HALF = 512
QUARTER = 256
W8_ROW = 4
SCALAR_SHARE = 48
PARK_SHARE = 64
LAST_SHARE = 42
SECOND_SHARE = 80
HIGH_SHARE = 160


def tile_mix_three_tm_pl_bias_kernel(
    tc, x, w8_words, w8_scales, w4_words, w4_scales, down, up_words, up_scales, b, out_0, out_1, out_2
):
    nc = tc.nc
    with ExitStack() as ctx:
        keep = ctx.enter_context(tc.tile_pool(name="keep", bufs=1))
        stage = ctx.enter_context(tc.tile_pool(name="stage", bufs=3))
        psum = ctx.enter_context(tc.psum_pool(name="psum", bufs=1))
        ctx.enter_context(tc.manual_schedule())

        def kept(name, shape, dtype):
            return keep.tile(shape, dtype, name=name, align_bytes=64)

        x_raw = [kept("x_raw%d" % g, [P, PACK, T], F32) for g in range(PASSES)]
        d_raw = [kept("d_raw%d" % g, [P, PACK, R], F32) for g in range(PASSES)]
        x_codes = [kept("x_codes%d" % g, [P, T], U32) for g in range(PASSES)]
        x_plane = [kept("x_plane%d" % g, [P, T], U8) for g in range(PASSES)]
        d_codes = [kept("d_codes%d" % g, [P, R], U32) for g in range(PASSES)]
        d_plane = [kept("d_plane%d" % g, [P, R], U8) for g in range(PASSES)]
        w8_low = [kept("w8_low%d" % g, [P, HALF], U32) for g in range(PASSES8)]
        w8_high = kept("w8_high", [P, PASSES8, HALF], U32)
        w4_first = kept("w4_first", [P, PASSES4 - 1, 2 * M], U8)
        w4_last = kept("w4_last", [P, 2 * M], U8)
        w4_codes = [w4_first[:, 0, :], w4_first[:, 1, :], w4_last[:]]
        up_codes = kept("up_codes", [P, 2 * M], U8)
        w8_plane = [kept("w8_plane%d" % h, [P, PASSES8, HALF], U8) for h in range(2)]
        w4_plane = kept("w4_plane", [P, PASSES4, M], U8)
        up_plane = kept("up_plane", [P, 1, M], U8)
        ident = kept("ident", [P, P], F32)
        b_cols = kept("b_cols", [P, 2 * PACK], F32)
        bias = kept("bias", [P, M], F32)
        parked = kept("parked", [P, PACK, HALF], F32)
        h_grouped = [kept("h_grouped%d" % i, [P, P, PACK], BF16) for i in range(PACK)]
        h_codes = kept("h_codes", [P, T], U32)
        h_plane = kept("h_plane", [P, T], U8)
        result = [kept("result%d" % h, [P, PACK, HALF], F32) for h in range(2)]
        o_grouped = [kept("o_grouped%d" % h, [P, HALF, PACK], BF16) for h in range(2)]
        o_codes = kept("o_codes", [P, M], U32)
        o_plane = kept("o_plane", [P, M], U8)

        def cols(n, width):
            return slice(n * width, (n + 1) * width)

        def load_rows(raw, src, g, queue=nc.sync):
            queue.dma_start(out=raw[g][:], in_=src[cols(g, K_PASS), :].rearrange("(p j) w -> p j w", j=PACK))

        w8_view = w8_words.rearrange("a p n i -> p a (n i)")

        def load_plane(plane, scales, n_cols=slice(0, M), row=0):
            rows = scales.rearrange("a (q r) n -> r q a n", r=4)
            for r in range(4):
                nc.sync.dma_start(out=plane[:].bitcast(I32)[row + r : P : 32], in_=rows[r][:, :, n_cols].bitcast(I32))

        def cast_and_deal(raw, share):
            grouped = stage.tile([P, PACK, P, PACK], BF16, name="grouped", align_bytes=64)
            dst = grouped[:].rearrange("p i m j -> p m j i")
            src = raw[:].rearrange("p j (m i) -> p m j i", i=PACK)
            nc.scalar.copy(out=dst[:, :share], in_=src[:, :share])
            nc.vector.tensor_copy(out=dst[:, share:], in_=src[:, share:])
            return grouped[:].rearrange("p i m j -> p (i m j)")

        def quantize(codes, plane, grouped, first, width):
            nc.vector.quantize_mx(
                out=codes[:, first : first + width].bitcast(FP8X4),
                scales=plane[:, first : first + width],
                in_=grouped,
            )

        def interleave(copy, h, first, width):
            copy(
                out=o_grouped[h][:, first : first + width, :].rearrange("p (c u) j -> p c j u", u=4),
                in_=result[h][:, :, first : first + width].rearrange("p j (c u) -> p c j u", u=4),
            )

        def quantize_out(h, first, width):
            grouped = o_grouped[h][:, first : first + width, :].rearrange("p c j -> p (c j)")
            quantize(o_codes, o_plane, grouped, h * HALF + first, width)

        def w4_pass(acc, g, i, h, start, stop):
            nc.tensor.matmul_mx(
                out=acc[:],
                lhsT=x_codes[g][:, cols(i, P)].bitcast(FP8X4),
                lhsT_scale=x_plane[g][:, cols(i, P)],
                rhs=w4_codes[g - PASSES8][:, cols(h, 2 * HALF)].bitcast(FP4X4),
                rhs_scale=w4_plane[:, g - PASSES8, cols(h, HALF)],
                start=start,
                stop=stop,
            )

        def w8_pass(out, g, i, words, first, width, start):
            nc.tensor.matmul_mx(
                out=out,
                lhsT=x_codes[g][:, cols(i, P)].bitcast(FP8X4),
                lhsT_scale=x_plane[g][:, cols(i, P)],
                rhs=words.bitcast(FP8X4),
                rhs_scale=w8_plane[first // HALF][W8_ROW:, g, first % HALF : first % HALF + width],
                start=start,
                stop=False,
            )

        def up_pass(out, i, first, width, stop):
            nc.tensor.matmul_mx(
                out=out,
                lhsT=h_codes[:, cols(i, P)].bitcast(FP8X4),
                lhsT_scale=h_plane[:, cols(i, P)],
                rhs=up_codes[:, 2 * first : 2 * (first + width)].bitcast(FP4X4),
                rhs_scale=up_plane[:, 0, first : first + width],
                start=False,
                stop=stop,
            )

        def h_pass(g, i, j):
            nc.tensor.matmul_mx(
                out=h_acc[i][:, j, :],
                lhsT=d_codes[g][:, cols(j, P)].bitcast(FP8X4),
                lhsT_scale=d_plane[g][:, cols(j, P)],
                rhs=x_codes[g][:, cols(i, P)].bitcast(FP8X4),
                rhs_scale=x_plane[g][:, cols(i, P)],
                start=(g == PASSES8 and j == 0),
                stop=(g == 1 and j == PACK - 1),
            )

        def add(out, acc, other):
            nc.vector.tensor_tensor(out=out, in0=acc, in1=other, op=mybir.AluOpType.add)

        out_rows = out_0.rearrange("(p i) n -> p i n", i=PACK)
        out_words = out_1[0].rearrange("p n i -> p (n i)").bitcast(I32)

        def store_words(first, width):
            nc.sync.dma_start(
                out=out_words[:, first : first + width], in_=o_codes[:, first : first + width].bitcast(I32)
            )

        nc.scalar.dma_start(out=b_cols[:], in_=b.rearrange("(p c) -> p c", p=P))
        make_identity(nc, ident[:])
        for plane in (w4_plane, w8_plane[0], up_plane, w8_plane[1]):
            nc.vector.memset(plane[:].bitcast(I32), 0)

        load_rows(x_raw, x, 2)
        w4_rows = w4_words.rearrange("a p c -> p a c")
        nc.scalar.dma_start(out=w4_first[:].bitcast(I32), in_=w4_rows[:, : PASSES4 - 1, :].bitcast(I32))
        load_rows(x_raw, x, 3, nc.scalar)
        load_plane(w4_plane, w4_scales)
        load_rows(x_raw, x, 4)
        nc.sync.dma_start(out=w4_last[:].bitcast(I32), in_=w4_words[PASSES4 - 1].bitcast(I32))
        load_rows(x_raw, x, 0, nc.scalar)
        load_plane(w8_plane[0], w8_scales, cols(0, HALF), W8_ROW)
        load_rows(d_raw, down, 1)

        def load_the_rest():
            load_rows(d_raw, down, 4, nc.scalar)
            load_rows(d_raw, down, 0)
            load_rows(x_raw, x, 1)
            nc.sync.dma_start(out=w8_low[0][:].bitcast(I32), in_=w8_view[:, 0, cols(0, PACK * HALF)].bitcast(I32))
            load_plane(up_plane, up_scales)
            nc.sync.dma_start(out=w8_low[1][:].bitcast(I32), in_=w8_view[:, 1, cols(0, PACK * HALF)].bitcast(I32))
            nc.sync.dma_start(out=up_codes[:].bitcast(I32), in_=up_words[0].bitcast(I32))
            nc.sync.dma_start(out=w8_high[:].bitcast(I32), in_=w8_view[:, :, cols(1, PACK * HALF)].bitcast(I32))
            load_plane(w8_plane[1], w8_scales, cols(1, HALF), W8_ROW)

        spread = [psum.tile([P, PACK, P], F32, name="spread%d" % h, tag="bank%d" % (4 + h)) for h in range(2)]
        for h in range(2):
            for c in range(PACK):
                nc.tensor.transpose(spread[h][:, c, :], b_cols[:, PACK * h + c : PACK * h + c + 1].to_broadcast([P, P]), ident[:])

        y_low = [psum.tile([P, HALF], F32, name="y_low%d" % i, tag="bank%d" % i) for i in range(PACK)]
        y_early = []
        for g in range(PASSES8, PASSES):
            if g == PASSES - 1:
                load_rows(d_raw, down, 2, nc.scalar)
                load_rows(d_raw, down, 3)
            grouped = cast_and_deal(x_raw[g], SCALAR_SHARE)
            quantize(x_codes[g], x_plane[g], grouped, 0, T)
            if g == PASSES8:
                for h, copy in enumerate((nc.scalar.copy, nc.vector.tensor_copy)):
                    copy(
                        out=bias[:].rearrange("t (p h c) -> t h p c", h=2, c=PACK)[:, h],
                        in_=spread[h][:].rearrange("t c p -> t p c"),
                    )
                y_early = [psum.tile([P, HALF], F32, name="y_early%d" % i, tag="bank%d" % (4 + i)) for i in range(PACK)]
            for i in range(PACK):
                w4_pass(y_early[i], g, i, 1, g == PASSES8, g == PASSES - 1)
            for i in range(PACK):
                w4_pass(y_low[i], g, i, 0, g == PASSES8, False)

        load_the_rest()
        for n, (raw, codes, plane) in enumerate(((x_raw[0], x_codes[0], x_plane[0]), (d_raw[1], d_codes[1], d_plane[1]))):
            grouped = cast_and_deal(raw, PARK_SHARE)
            for i in (2 * n, 2 * n + 1):
                add(parked[:, i, :], y_early[i][:], bias[:, cols(1, HALF)])
            quantize(codes, plane, grouped, 0, T)

        h_acc = [psum.tile([P, PACK, P], F32, name="h_acc%d" % i, tag="bank%d" % (4 + i)) for i in range(PACK)]
        for g in range(PASSES8, PASSES):
            grouped = cast_and_deal(d_raw[g], SCALAR_SHARE)
            quantize(d_codes[g], d_plane[g], grouped, 0, R)
            for i in range(PACK):
                for j in range(PACK):
                    h_pass(g, i, j)
        grouped = cast_and_deal(d_raw[0], LAST_SHARE)
        for j in range(PACK):
            quantize(d_codes[0], d_plane[0], grouped[:, cols(j, K_PASS)], j * P, P)
            for i in range(PACK):
                h_pass(0, i, j)
        last = kept("last_grouped", [P, PACK, P, PACK], BF16)
        last_dst = last[:].rearrange("p i m j -> p m j i")
        last_src = x_raw[1][:].rearrange("p j (m i) -> p m j i", i=PACK)

        def cast_slots(copy, ms, pair):
            copy(out=last_dst[:, ms, :, cols(pair, 2)], in_=last_src[:, ms, :, cols(pair, 2)])

        def quantize_slot(i):
            quantize(x_codes[1], x_plane[1], last[:, i].rearrange("p m j -> p (m j)"), i * P, P)

        def low_w8(i, g):
            w8_pass(y_low[i][:], g, i, w8_low[g][:], 0, HALF, False)

        def low_up(i):
            up_pass(y_low[i][:], i, 0, HALF, True)

        def h_close(i):
            for j in range(PACK):
                h_pass(1, i, j)

        def h_out(copy, i):
            copy(
                out=h_grouped[i][:].rearrange("p (c u) j -> p c j u", u=4),
                in_=h_acc[i][:].rearrange("p j (c u) -> p c j u", u=4),
            )

        def h_quantize(i):
            quantize(h_codes, h_plane, h_grouped[i][:].rearrange("p t j -> p (t j)"), i * P, P)

        def add_low(i, first, width):
            c = slice(first, first + width)
            add(result[0][:, i, c], y_low[i][:, c], bias[:, c])
            if first + width == HALF:
                nc.sync.dma_start(out=out_rows[:, i, cols(0, HALF)], in_=result[0][:, i, :])

        def high_tile(bank, n, width):
            return psum.tile([P, n, width], F32, name="y_high%d" % bank, tag="bank%d" % bank)

        def high_w8(acc, slots, first, width):
            for g in range(PASSES8):
                for e, i in enumerate(slots):
                    w8_pass(acc[:, e, :], g, i, w8_high[:, g, first : first + width], HALF + first, width, g == 0 and e == 0)

        def high_up(acc, slots, first, width):
            step = HALF if width == HALF else P
            for e, i in enumerate(slots):
                for u in range(0, width, step):
                    up_pass(acc[:, e, u : u + step], i, HALF + first + u, step, e == len(slots) - 1 and u + step == width)

        def add_high(acc, slots, first, width):
            rows, c = slice(slots[0], slots[-1] + 1), slice(first, first + width)
            add(result[1][:, rows, c], acc[:], parked[:, rows, c])

        def high_bank(bank, slots, first, width):
            acc = high_tile(bank, len(slots), width)
            high_w8(acc, slots, first, width)
            high_up(acc, slots, first, width)
            return acc

        def store_high(rows, first, width):
            nc.sync.dma_start(
                out=out_rows[:, rows, HALF + first : HALF + first + width], in_=result[1][:, rows, first : first + width]
            )

        def G(out, in_):
            nc.gpsimd.tensor_scalar(
                out=out, in0=in_, scalar1=1.0, scalar2=0.0, op0=mybir.AluOpType.mult, op1=mybir.AluOpType.add
            )

        S, V = nc.scalar.copy, nc.vector.tensor_copy
        cast_slots(S, slice(0, LAST_SHARE), 0)
        cast_slots(V, slice(LAST_SHARE, P), 0)
        cast_slots(S, slice(0, SECOND_SHARE), 1)
        quantize_slot(0)
        quantize_slot(1)
        cast_slots(V, slice(SECOND_SHARE, P), 1)
        low_w8(0, 0)
        low_w8(1, 0)
        h_close(0)
        h_close(1)
        h_out(S, 0)
        quantize_slot(2)
        quantize_slot(3)
        h_out(V, 1)
        low_w8(0, 1)
        h_close(2)
        h_out(S, 2)
        h_close(3)
        h_quantize(0)
        h_quantize(1)
        low_w8(1, 1)
        low_up(0)
        low_up(1)
        h_out(S, 3)
        h_quantize(2)
        add_low(0, 0, HALF)
        low_w8(2, 0)
        low_w8(2, 1)
        low_up(2)
        h_quantize(3)
        add_low(1, 0, HALF)
        low_w8(3, 0)
        low_w8(3, 1)
        low_up(3)
        add_low(2, 0, HALF)
        add_low(3, 0, QUARTER)
        interleave(S, 0, 0, QUARTER)
        add_low(3, QUARTER, QUARTER)
        interleave(G, 0, QUARTER + P, P)
        interleave(S, 0, QUARTER, P)
        for i in range(2):
            acc = high_bank(4 + i, (i,), 0, HALF)
            add_high(acc, (i,), 0, HALF)
            store_high(slice(i, i + 1), 0, HALF)
        quantize_out(0, 0, QUARTER)
        store_words(0, QUARTER)
        acc = high_bank(6, (2, 3), 0, QUARTER)
        add_high(acc, (2, 3), 0, QUARTER)
        store_high(slice(2, 4), 0, QUARTER)
        interleave(S, 1, 0, HIGH_SHARE)
        acc = high_bank(7, (2, 3), QUARTER, P)
        add_high(acc, (2, 3), QUARTER, P)
        interleave(S, 1, QUARTER, P)
        interleave(V, 1, HIGH_SHARE, QUARTER - HIGH_SHARE)
        acc = high_bank(0, (2, 3), QUARTER + P, P)
        add_high(acc, (2, 3), QUARTER + P, P)
        store_high(slice(2, 4), QUARTER, QUARTER)
        quantize_out(0, QUARTER, QUARTER)
        quantize_out(1, 0, QUARTER)
        store_words(QUARTER, HALF)
        interleave(V, 1, QUARTER + P, P)
        quantize_out(1, QUARTER, P)
        quantize_out(1, QUARTER + P, P)
        store_words(HALF + QUARTER, QUARTER)
        for q in range(4):
            queue = nc.sync if q < 2 else nc.scalar
            queue.dma_start(
                out=out_2[0, 4 * q : 4 * q + 4, :].bitcast(I32), in_=o_plane[:].bitcast(I32)[32 * q : 32 * q + 4, :]
            )
